import numpy as np
import ml_dtypes


def mxq(x, axis, fmt="e4m3"):
    dtype, down = {"e4m3": (ml_dtypes.float8_e4m3fn, 7), "e5m2": (ml_dtypes.float8_e5m2, 14)}[fmt]
    v = np.moveaxis(np.asarray(x, np.float32).astype(ml_dtypes.bfloat16).astype(np.float64), axis, -1)
    blocks = v.reshape(v.shape[:-1] + (-1, 32))
    amax = np.abs(blocks).max(-1, keepdims=True)
    byte = np.maximum(np.where(amax > 0, np.frexp(amax)[1] - 1 + 127, 0) - down, 1)
    scale = np.exp2(byte - 127.0)
    codes = (blocks / scale).astype(np.float32).astype(dtype).astype(np.float64)
    return np.moveaxis((codes * scale).reshape(v.shape), -1, axis)


WIDE = False


def mx_kscale(k):
    if not WIDE:
        return np.ones(k)
    levels = np.array([24, -24, 12, -12, 0])
    if k % 512:
        return np.exp2(np.random.permutation(np.resize(levels, k // 32))).repeat(32)
    a = np.empty((k // 512, 16))
    for p in range(k // 512):
        a[p, :8] = np.random.permutation(np.resize(levels, 8))
        for g in range(8):
            far = levels[np.abs(levels - a[p, g]) >= 10]
            a[p, g + 8] = far[np.random.randint(len(far))]
    return np.exp2(a.ravel()).repeat(32)


def f64(x):
    return np.asarray(x).astype(np.float64)


def striped(idx):
    return np.tile(idx.reshape(-1, 16).T, (8, 1)).astype(np.uint16)


def unstriped(offs):
    return offs[:16].T.reshape(-1).astype(np.int64)


E2M1 = np.array([0.0, 0.5, 1.0, 1.5, 2.0, 3.0, 4.0, 6.0, -0.0, -0.5, -1.0, -1.5, -2.0, -3.0, -4.0, -6.0])


def pack_weight(w, fmt):
    k, n = w.shape
    w = f64(np.asarray(w, np.float32).astype(ml_dtypes.bfloat16)).reshape(k // 32, 32, n)
    amax = np.abs(w).max(1)
    if fmt == "e4m3":
        byte = np.frexp(amax)[1] - 1 + 127 - 7
    else:
        mant, ex = np.frexp(amax / 6.0)
        byte = np.where(mant > 0.5, ex, ex - 1) + 127
    byte = np.clip(np.where(amax > 0, byte, 1), 1, 254)
    scaled = (w * np.exp2(127.0 - byte)[:, None, :]).reshape(k, n).astype(np.float32)
    by_word = np.ascontiguousarray(scaled.reshape(k // 512, 128, 4, n).transpose(0, 1, 3, 2))
    if fmt == "e4m3":
        words = by_word.astype(ml_dtypes.float8_e4m3fn).view(np.uint8)
    else:
        c = by_word.astype(ml_dtypes.float4_e2m1fn).view(np.uint8) & 0xF
        words = (c[..., 0::2] | (c[..., 1::2] << 4)).reshape(k // 512, 128, 2 * n)
    return np.ascontiguousarray(words), np.ascontiguousarray(byte.astype(np.uint8).reshape(k // 512, 16, n))


def unpack_weight(words, scales, fmt):
    g, _, n = scales.shape
    words = np.ascontiguousarray(words).reshape(g, 128, n, -1)
    if fmt == "e4m3":
        vals = words.view(ml_dtypes.float8_e4m3fn).astype(np.float64)
    else:
        nib = np.empty((g, 128, n, 4), np.uint8)
        nib[..., 0::2] = words & 0xF
        nib[..., 1::2] = words >> 4
        vals = E2M1[nib]
    vals = vals * np.repeat(np.exp2(scales.astype(np.float64) - 127.0), 8, axis=1)[..., None]
    return vals.transpose(0, 1, 3, 2).reshape(g * 512, n)


def pack_table4(v):
    words, scales = pack_weight(v, "e2m1")
    g, t = words.shape[0] // 2, v.shape[1]
    return np.ascontiguousarray(words.reshape(g, 2, 128, t, 2).transpose(0, 2, 3, 1, 4).reshape(g, 128, t, 4)), scales


def unpack_table4(words, scales):
    g, _, t, _ = words.shape
    return unpack_weight(words.reshape(g, 128, t, 2, 2).transpose(0, 3, 1, 2, 4).reshape(2 * g, 128, 2 * t), scales, "e2m1")


K, R, M, N, T, J = 1024, 1024, 512, 256, 4096, 1024


def setup_inputs():
    n = np.random.standard_normal
    s = mx_kscale(K)[:, None]
    s2 = mx_kscale(K)[:, None]
    u = mx_kscale(R)[:, None]
    p_tab = pack_table4(n((K, T)) * s2)
    p_wk = pack_weight(n((K, R)) / np.sqrt(K) / s2 * u.T, "e4m3")
    return {
        "tab_words": p_tab[0],
        "tab_scales": p_tab[1],
        "x": (n((K, M)) * s).astype(np.float32),
        "wq": (n((K, R)) / np.sqrt(K) / s / u.T).astype(np.float32),
        "wk_words": p_wk[0],
        "wk_scales": p_wk[1],
        "wv": (n((K, N)) / np.sqrt(K) / s2).astype(np.float32),
        "ts": np.tile(np.exp(0.5 * n(T)) / 32.0, (128, 1)).astype(np.float32),
        "offs": striped(np.random.permutation(T)[:J]),
    }


def reference(tab_words, tab_scales, x, wq, wk_words, wk_scales, wv, ts, offs):
    idx = unstriped(offs)
    tab_ = unpack_table4(tab_words, tab_scales)[:, idx]
    x_ = mxq(f64(x), 0, "e4m3")
    wq_ = mxq(f64(wq), 0, "e4m3")
    wk_ = unpack_weight(wk_words, wk_scales, "e4m3")
    qr = wq_.T @ x_
    kr = wk_.T @ tab_
    qr_ = mxq(qr, 0, "e4m3")
    kr_ = mxq(kr, 0, "e4m3")
    sc = qr_.T @ kr_
    wv_ = mxq(f64(wv), 0, "e4m3")
    vv = wv_.T @ tab_
    return sc * f64(ts)[0, idx][None, :], vv

@@ -1,0 +1,304 @@
+from contextlib import ExitStack
+
+import concourse.mybir as mybir
+from concourse.masks import make_identity
+
+K, R, M, N, T, J = 1024, 1024, 512, 256, 4096, 1024
+FLOPS = 2 * (K * R * M + K * R * J + R * M * J + K * N * J)
+
+F32 = mybir.dt.float32
+BF16 = mybir.dt.bfloat16
+I32 = mybir.dt.int32
+U32 = mybir.dt.uint32
+U16 = mybir.dt.uint16
+U8 = mybir.dt.uint8
+FP8X4 = mybir.dt.float8_e4m3fn_x4
+FP4X4 = mybir.dt.float4_e2m1fn_x4
+MULT = mybir.AluOpType.mult
+
+P = 128
+PACK = 4
+KP = P * PACK
+BANK = 512
+
+
+def tile_list_kvt_ts_kernel(
+    tc, tab_words, tab_scales, x, wq, wk_words, wk_scales, wv, ts, offs, out_0, out_1
+):
+    nc = tc.nc
+    with ExitStack() as ctx:
+        sb = ctx.enter_context(tc.tile_pool(name="sb", bufs=1))
+        psum = ctx.enter_context(tc.psum_pool(name="psum", bufs=8))
+
+        def tile(name, shape, dtype, tag=None):
+            return sb.tile(shape, dtype, name=name, tag=tag or name, align_bytes=64)
+
+        def bank(shape):
+            return psum.tile(shape, F32, name="bank")
+
+        offsets = tile("offsets", [P, J // 16], U16)
+        nc.sync.dma_start(offsets[:], offs)
+
+        ts_row = tile("ts_row", [P, T // P], F32)
+        nc.scalar.dma_start(ts_row[:], ts[0, :].rearrange("(n c) -> n c", n=P))
+        ident = tile("ident", [P, P], F32)
+        make_identity(nc, ident[:])
+        tab_sc = tile("tab_sc", [P, T], U8, "slot0")
+        wk_sc_raw = tile("wk_sc_raw", [P, 2, R], U8)
+        v_sc1 = tile("v_sc1", [P, J], U8)
+        nc.vector.memset(tab_sc[:].bitcast(I32), 0)
+        nc.vector.memset(wk_sc_raw[:].rearrange("p a r -> p (a r)").bitcast(I32), 0)
+        nc.vector.memset(v_sc1[:].bitcast(I32), 0)
+
+        wk_src = wk_words.rearrange("a p r i -> p a (r i)")
+        wk_raw00 = tile("wk_raw00", [P, KP], I32, "slot1")
+        wk_raw10 = tile("wk_raw10", [P, KP], I32)
+        wk_raw1 = tile("wk_raw1", [P, 2, KP], I32)
+        nc.sync.dma_start(wk_raw00[:], wk_src[:, 0, 0 : 4 * KP].bitcast(I32))
+        nc.sync.dma_start(wk_raw10[:], wk_src[:, 1, 0 : 4 * KP].bitcast(I32))
+        nc.sync.dma_start(wk_raw1[:], wk_src[:, :, 4 * KP : 8 * KP].bitcast(I32))
+        tab_rows = tab_scales.rearrange("a (q r) t -> r q a t", r=4)
+        for r in range(4):
+            nc.scalar.dma_start(tab_sc[r:P:16, :].bitcast(I32), tab_rows[r].bitcast(I32))
+        wk_rows = wk_scales.rearrange("a (q r) n -> r q a n", r=4)
+        for r in range(4):
+            queue = nc.scalar if r < 1 else nc.gpsimd
+            queue.dma_start(wk_sc_raw[r:P:32, :, :].bitcast(I32), wk_rows[r].bitcast(I32))
+
+        def load_rows(name, src, a, cols, tag):
+            raw = tile(name, [P, PACK, cols.stop - cols.start], F32, tag)
+            nc.sync.dma_start(raw[:], src[a * KP : (a + 1) * KP, cols].rearrange("(p i) c -> p i c", i=PACK))
+            return raw
+
+        ts_win = tile("ts_win", [P, T], F32, "slot2")
+        ts_by_n = ts_win[:].rearrange("p (n c) -> p n c", n=P)
+        for g in range(T // P // 4):
+            acc = bank([P, 4, P])
+            for c in range(4):
+                col = 4 * g + c
+                nc.tensor.transpose(acc[:, c, :], ts_row[:, col : col + 1].to_broadcast([P, P]), ident[:])
+            nc.scalar.copy(ts_by_n[:, :, 4 * g : 4 * g + 4], acc[:].rearrange("p c n -> p n c"))
+
+        wk_q = [tile("wk_q%d" % b, [P, 2, KP], I32) for b in range(2)]
+
+        def order_wk(out, raw):
+            nc.vector.tensor_copy(
+                out.rearrange("p (s t g i) -> p s t g i", t=4, g=16, i=8),
+                raw.rearrange("p (s g t i) -> p s t g i", t=4, g=16, i=8),
+            )
+
+        order_wk(wk_q[0][:, 0, :], wk_raw00[:])
+        tab_w = tile("tab_w", [P, T], U32, "slot1")
+        nc.sync.dma_start(tab_w[:].bitcast(I32), tab_words[0].rearrange("p t b -> p (t b)").bitcast(I32))
+        order_wk(wk_q[0][:, 1, :], wk_raw10[:])
+        v_sc0 = tile("v_sc0", [P, J], U8)
+        nc.vector.tensor_copy(v_sc0[:], tab_sc[:].indirect(offsets[:]))
+        nc.sync.dma_start(v_sc1[0 : P - 16, :].bitcast(I32), v_sc0[16:P, :].bitcast(I32))
+        v_sc = [v_sc0, v_sc1]
+
+        wk_sc = tile("wk_sc", [P, 2, R], U8)
+        nc.vector.tensor_copy(
+            wk_sc[:].rearrange("p a r -> p (a r)").bitcast(I32).rearrange("p (s t g h) -> p s t g h", t=4, g=16, h=2),
+            wk_sc_raw[:].rearrange("p a r -> p (a r)").bitcast(I32).rearrange("p (s g t h) -> p s t g h", t=4, g=16, h=2),
+        )
+        order_wk(wk_q[1][:].rearrange("p a r -> p (a r)"), wk_raw1[:].rearrange("p a r -> p (a r)"))
+
+        v_pair = {}
+        v_q = [tile("v_q%d" % h, [P, 2, BANK], U16) for h in range(2)]
+
+        def gather_words(h):
+            v_pair[h] = tile("v_pair%d" % h, [P, BANK], U32, "slot3")
+            nc.vector.tensor_copy(v_pair[h][:], tab_w[:].indirect(offsets[:, 32 * h : 32 * (h + 1)]))
+
+        def part_words(h):
+            nc.vector.tensor_copy(v_q[h][:], v_pair[h][:].bitcast(U16).rearrange("p (j d) -> p d j", d=2))
+
+        def quantize(name, rounded, cols):
+            codes = tile(name + "_q", [P, cols], U32)
+            scales = tile(name + "_s", [P, cols], U8)
+            nc.vector.quantize_mx(out=codes[:].bitcast(FP8X4), scales=scales[:], in_=rounded)
+            return codes, scales
+
+        def copy_on(engine, out, in_):
+            if engine == "scalar":
+                nc.scalar.copy(out, in_)
+            else:
+                nc.vector.tensor_copy(out, in_)
+
+        def round_plain(name, raw, cols, engine, tag=None):
+            rounded = tile(name + "_bf", [P, cols * PACK], BF16, tag)
+            copy_on(
+                engine,
+                rounded[:].rearrange("p (c u i) -> p c i u", u=4, i=PACK),
+                raw.rearrange("p i (c u) -> p c i u", u=4),
+            )
+            return rounded
+
+        def round_wq(a, b, engine, t0=0, t1=4):
+            rounded = tile("wq%d%d%d_bf" % (a, b, t0), [P, (t1 - t0) * P * PACK], BF16)
+            copy_on(
+                engine,
+                rounded[:].rearrange("p (t g u i) -> p t g i u", g=16, u=8, i=PACK),
+                wq_raw[a, b][:].rearrange("p i (g t u) -> p t g i u", t=4, u=8)[:, t0:t1],
+            )
+            return rounded
+
+        def quantize_wq(a, b, rounded, t0=0, t1=4):
+            codes, scales = quantize("wq%d%d%d" % (a, b, t0), rounded[:], (t1 - t0) * P)
+            for t in range(t0, t1):
+                cols = slice((t - t0) * P, (t - t0 + 1) * P)
+                wq_q[a, b, t] = (codes[:, cols], scales[:, cols])
+
+        kr_bf = {(b, h): tile("kr_bf%d%d" % (b, h), [P, BANK, PACK], BF16) for b in range(2) for h in range(2)}
+
+        def kr_bank(b, h, c):
+            acc = bank([P, 4, P])
+            cols = slice(c * P, (c + 1) * P)
+            jcols = slice(h * BANK + c * P, h * BANK + (c + 1) * P)
+            for t in range(4):
+                for a in range(2):
+                    nc.tensor.matmul_mx(
+                        out=acc[:, t, :],
+                        lhsT=wk_q[b][:, a, t * P : (t + 1) * P].bitcast(FP8X4),
+                        lhsT_scale=wk_sc[:, a, b * KP + t * P : b * KP + (t + 1) * P],
+                        rhs=v_q[h][:, a, cols].bitcast(FP4X4),
+                        rhs_scale=v_sc[a][:, jcols],
+                        start=(a == 0),
+                        stop=(a == 1),
+                    )
+            nc.scalar.copy(kr_bf[b, h][:, cols, :], acc[:].rearrange("p t n -> p n t"))
+
+        kr_q = {}
+
+        def quantize_kr(b, h):
+            kr_q[b, h] = quantize("kr%d%d" % (b, h), kr_bf[b, h][:].rearrange("p n t -> p (n t)"), BANK)
+
+        x_q = {}
+        wq_q = {}
+        wq_raw = {}
+        half = [slice(0, KP), slice(KP, 2 * KP)]
+        x_raw = tile("x_raw", [P, 2, PACK, M], F32, "slot0")
+        nc.sync.dma_start(x_raw[:].rearrange("p a i c -> p a (i c)"), x.rearrange("(a p i) c -> p a (i c)", a=2, i=PACK))
+        gather_words(0)
+        part_words(0)
+        gather_words(1)
+        wq_raw[0, 0] = load_rows("wq_raw00", wq, 0, half[0], "slot1")
+        for b in range(2):
+            for c in range(4):
+                kr_bank(b, 0, c)
+        part_words(1)
+        wq_raw[1, 0] = load_rows("wq_raw10", wq, 1, half[0], "slot3")
+        ts_g = tile("ts_g", [P, J], F32)
+        nc.vector.tensor_copy(ts_g[:], ts_win[:].indirect(offsets[:]))
+        wq_raw[0, 1] = load_rows("wq_raw01", wq, 0, half[1], "slot2")
+
+        x_bf0 = round_plain("x0", x_raw[:, 0], M, "vector")
+        x_bf1 = round_plain("x1", x_raw[:, 1], M, "scalar", "slot4")
+        wq_raw[1, 1] = load_rows("wq_raw11", wq, 1, half[1], "slot0")
+        quantize_kr(0, 0)
+        x_q[0] = quantize("x0", x_bf0[:], M)
+        wq_bf00 = round_wq(0, 0, "vector")
+        x_q[1] = quantize("x1", x_bf1[:], M)
+        wv_raw = tile("wv_raw", [P, 2, PACK, N], F32, "slot4")
+        nc.sync.dma_start(wv_raw[:].rearrange("p a i c -> p a (i c)"), wv.rearrange("(a p i) c -> p a (i c)", a=2, i=PACK))
+        quantize_wq(0, 0, wq_bf00)
+        for b in range(2):
+            for c in range(4):
+                kr_bank(b, 1, c)
+        wq_bf10 = round_wq(1, 0, "vector")
+        quantize_kr(1, 0)
+        quantize_wq(1, 0, wq_bf10)
+        wq_bf01 = round_wq(0, 1, "vector")
+        quantize_kr(0, 1)
+
+        qr_bf = [tile("qr_bf%d" % m, [P, 2, P, PACK], BF16) for m in range(4)]
+
+        def qr_bank(b, m):
+            acc = bank([P, 4, P])
+            cols = slice(m * P, (m + 1) * P)
+            for t in range(4):
+                for a in range(2):
+                    nc.tensor.matmul_mx(
+                        out=acc[:, t, :],
+                        lhsT=wq_q[a, b, t][0].bitcast(FP8X4),
+                        lhsT_scale=wq_q[a, b, t][1],
+                        rhs=x_q[a][0][:, cols].bitcast(FP8X4),
+                        rhs_scale=x_q[a][1][:, cols],
+                        start=(a == 0),
+                        stop=(a == 1),
+                    )
+            nc.scalar.copy(qr_bf[m][:, b, :, :], acc[:].rearrange("p t n -> p n t"))
+
+        for m in range(4):
+            qr_bank(0, m)
+        quantize_wq(0, 1, wq_bf01)
+        wq_bf11a = round_wq(1, 1, "vector", 0, 2)
+        wq_bf11b = round_wq(1, 1, "scalar", 2, 4)
+        quantize_kr(1, 1)
+        quantize_wq(1, 1, wq_bf11a, 0, 2)
+        quantize_wq(1, 1, wq_bf11b, 2, 4)
+
+        qr_q = {}
+
+        def quantize_qr(m):
+            qr_q[m] = quantize("qr%d" % m, qr_bf[m][:].rearrange("p b n t -> p (b n t)"), 2 * P)
+
+        def scores(m):
+            res = tile("sc%d" % m, [P, J], F32)
+            for h in range(2):
+                acc = bank([P, BANK])
+                for b in range(2):
+                    nc.tensor.matmul_mx(
+                        out=acc[:],
+                        lhsT=qr_q[m][0][:, b * P : (b + 1) * P].bitcast(FP8X4),
+                        lhsT_scale=qr_q[m][1][:, b * P : (b + 1) * P],
+                        rhs=kr_q[b, h][0][:].bitcast(FP8X4),
+                        rhs_scale=kr_q[b, h][1][:],
+                        start=(b == 0),
+                        stop=(b == 1),
+                    )
+                cols = slice(h * BANK, (h + 1) * BANK)
+                nc.vector.tensor_tensor(res[:, cols], acc[:], ts_g[:, cols], MULT)
+                if m == 3:
+                    nc.sync.dma_start(out_0[m * P : (m + 1) * P, cols], res[:, cols])
+            if m < 3:
+                nc.sync.dma_start(out_0[m * P : (m + 1) * P, :], res[:])
+
+        wv_q = {}
+
+        def values(n):
+            res = tile("vv%d" % n, [P, J], F32)
+            for h in range(2):
+                acc = bank([P, BANK])
+                cols = slice(h * BANK, (h + 1) * BANK)
+                for a in range(2):
+                    nc.tensor.matmul_mx(
+                        out=acc[:],
+                        lhsT=wv_q[a][0][:, n * P : (n + 1) * P].bitcast(FP8X4),
+                        lhsT_scale=wv_q[a][1][:, n * P : (n + 1) * P],
+                        rhs=v_q[h][:, a, :].bitcast(FP4X4),
+                        rhs_scale=v_sc[a][:, cols],
+                        start=(a == 0),
+                        stop=(a == 1),
+                    )
+                nc.scalar.copy(res[:, cols], acc[:])
+            nc.sync.dma_start(out_1[n * P : (n + 1) * P, :], res[:])
+
+        qr_bank(1, 0)
+        qr_bank(1, 1)
+        quantize_qr(0)
+        wv_bf0 = round_plain("wv0", wv_raw[:, 0], N, "scalar")
+        qr_bank(1, 2)
+        quantize_qr(1)
+        scores(0)
+        qr_bank(1, 3)
+        wv_bf1 = round_plain("wv1", wv_raw[:, 1], N, "scalar")
+        wv_q[0] = quantize("wv0", wv_bf0[:], N)
+        quantize_qr(2)
+        scores(1)
+        wv_q[1] = quantize("wv1", wv_bf1[:], N)
+        quantize_qr(3)
+        values(0)
+        scores(2)
+        values(1)
+        scores(3)

@@ -1,7 +1,6 @@
 from contextlib import ExitStack
 
 import concourse.mybir as mybir
-from concourse.masks import make_identity
 
 K, R, M, N, T, J = 1024, 1024, 512, 256, 4096, 1024
 FLOPS = 2 * (K * R * M + K * R * J + R * M * J + K * N * J)
@@ -28,80 +27,103 @@ def tile_list_kvt_ts_kernel(
     nc = tc.nc
     with ExitStack() as ctx:
         sb = ctx.enter_context(tc.tile_pool(name="sb", bufs=1))
+        shared = ctx.enter_context(tc.tile_pool(name="shared", bufs=1))
         psum = ctx.enter_context(tc.psum_pool(name="psum", bufs=8))
 
         def tile(name, shape, dtype, tag=None):
             return sb.tile(shape, dtype, name=name, tag=tag or name, align_bytes=64)
 
+        def placed(name, shape, dtype, offset):
+            return shared.tile(shape, dtype, name=name, offset=offset, align_bytes=64)
+
         def bank(shape):
             return psum.tile(shape, F32, name="bank")
+
+        def copy_on(engine, out, in_):
+            if engine == "scalar":
+                nc.scalar.copy(out, in_)
+            else:
+                nc.vector.tensor_copy(out, in_)
 
         offsets = tile("offsets", [P, J // 16], U16)
         nc.sync.dma_start(offsets[:], offs)
 
         ts_row = tile("ts_row", [P, T // P], F32)
         nc.scalar.dma_start(ts_row[:], ts[0, :].rearrange("(n c) -> n c", n=P))
-        ident = tile("ident", [P, P], F32)
-        make_identity(nc, ident[:])
-        tab_sc = tile("tab_sc", [P, T], U8, "slot0")
-        wk_sc_raw = tile("wk_sc_raw", [P, 2, R], U8)
-        v_sc1 = tile("v_sc1", [P, J], U8)
-        nc.vector.memset(tab_sc[:].bitcast(I32), 0)
-        nc.vector.memset(wk_sc_raw[:].rearrange("p a r -> p (a r)").bitcast(I32), 0)
-        nc.vector.memset(v_sc1[:].bitcast(I32), 0)
-
         wk_src = wk_words.rearrange("a p r i -> p a (r i)")
-        wk_raw00 = tile("wk_raw00", [P, KP], I32, "slot1")
-        wk_raw10 = tile("wk_raw10", [P, KP], I32)
-        wk_raw1 = tile("wk_raw1", [P, 2, KP], I32)
-        nc.sync.dma_start(wk_raw00[:], wk_src[:, 0, 0 : 4 * KP].bitcast(I32))
-        nc.sync.dma_start(wk_raw10[:], wk_src[:, 1, 0 : 4 * KP].bitcast(I32))
-        nc.sync.dma_start(wk_raw1[:], wk_src[:, :, 4 * KP : 8 * KP].bitcast(I32))
+        wk_raw0 = tile("wk_raw0", [P, 2, KP], I32)
+        nc.sync.dma_start(wk_raw0[:], wk_src[:, :, 0 : 4 * KP].bitcast(I32))
+
+        tab_sc = placed("tab_sc", [P, T], U8, 6144)
+        nc.vector.memset(tab_sc[:].bitcast(I32), 0)
         tab_rows = tab_scales.rearrange("a (q r) t -> r q a t", r=4)
         for r in range(4):
-            nc.scalar.dma_start(tab_sc[r:P:16, :].bitcast(I32), tab_rows[r].bitcast(I32))
+            nc.sync.dma_start(tab_sc[r:P:16, :].bitcast(I32), tab_rows[r].bitcast(I32))
+
+        ones = tile("ones", [P, P], F32, "slot1")
+        ident = tile("ident", [P, P], F32)
+        nc.gpsimd.memset(ones[:], 1.0)
+        nc.gpsimd.affine_select(
+            out=ident[:],
+            in_=ones[:],
+            pattern=[[-1, P]],
+            compare_op=mybir.AluOpType.is_equal,
+            fill=0.0,
+            base=0,
+            channel_multiplier=1,
+        )
+        tab_w = tile("tab_w", [P, T], U32, "slot1")
+        nc.sync.dma_start(tab_w[:].bitcast(I32), tab_words[0].rearrange("p t b -> p (t b)").bitcast(I32))
+
+        wk_sc_raw = tile("wk_sc_raw", [P, 2, R], U8, "slot0")
+        nc.gpsimd.memset(wk_sc_raw[:].rearrange("p a r -> p (a r)").bitcast(I32), 0)
         wk_rows = wk_scales.rearrange("a (q r) n -> r q a n", r=4)
         for r in range(4):
-            queue = nc.scalar if r < 1 else nc.gpsimd
-            queue.dma_start(wk_sc_raw[r:P:32, :, :].bitcast(I32), wk_rows[r].bitcast(I32))
+            nc.sync.dma_start(wk_sc_raw[r:P:32, :, :].bitcast(I32), wk_rows[r].bitcast(I32))
+        v_sc1 = tile("v_sc1", [P, J], U8)
+        nc.vector.memset(v_sc1[:].bitcast(I32), 0)
 
-        def load_rows(name, src, a, cols, tag):
-            raw = tile(name, [P, PACK, cols.stop - cols.start], F32, tag)
+        def load_rows(raw, src, a, cols):
             nc.sync.dma_start(raw[:], src[a * KP : (a + 1) * KP, cols].rearrange("(p i) c -> p i c", i=PACK))
             return raw
 
-        ts_win = tile("ts_win", [P, T], F32, "slot2")
+        ts_win = tile("ts_win", [P, T], F32)
         ts_by_n = ts_win[:].rearrange("p (n c) -> p n c", n=P)
         for g in range(T // P // 4):
             acc = bank([P, 4, P])
             for c in range(4):
                 col = 4 * g + c
                 nc.tensor.transpose(acc[:, c, :], ts_row[:, col : col + 1].to_broadcast([P, P]), ident[:])
-            nc.scalar.copy(ts_by_n[:, :, 4 * g : 4 * g + 4], acc[:].rearrange("p c n -> p n c"))
+            copy_on("vector" if g < 2 else "scalar", ts_by_n[:, :, 4 * g : 4 * g + 4], acc[:].rearrange("p c n -> p n c"))
 
         wk_q = [tile("wk_q%d" % b, [P, 2, KP], I32) for b in range(2)]
 
-        def order_wk(out, raw):
+        def order_wk(b, raw):
             nc.vector.tensor_copy(
-                out.rearrange("p (s t g i) -> p s t g i", t=4, g=16, i=8),
-                raw.rearrange("p (s g t i) -> p s t g i", t=4, g=16, i=8),
+                wk_q[b][:].rearrange("p a (t g i) -> p a t g i", t=4, i=8),
+                raw[:].rearrange("p a (g t i) -> p a t g i", t=4, i=8),
             )
 
-        order_wk(wk_q[0][:, 0, :], wk_raw00[:])
-        tab_w = tile("tab_w", [P, T], U32, "slot1")
-        nc.sync.dma_start(tab_w[:].bitcast(I32), tab_words[0].rearrange("p t b -> p (t b)").bitcast(I32))
-        order_wk(wk_q[0][:, 1, :], wk_raw10[:])
+        order_wk(0, wk_raw0)
         v_sc0 = tile("v_sc0", [P, J], U8)
-        nc.vector.tensor_copy(v_sc0[:], tab_sc[:].indirect(offsets[:]))
-        nc.sync.dma_start(v_sc1[0 : P - 16, :].bitcast(I32), v_sc0[16:P, :].bitcast(I32))
+        for h in range(2):
+            cols = slice(h * BANK, (h + 1) * BANK)
+            nc.vector.tensor_copy(v_sc0[:, cols], tab_sc[:].indirect(offsets[:, 32 * h : 32 * (h + 1)]))
+            nc.sync.dma_start(v_sc1[0 : P - 16, cols].bitcast(I32), v_sc0[16:P, cols].bitcast(I32))
         v_sc = [v_sc0, v_sc1]
+        x_raw0 = load_rows(placed("x_raw0", [P, PACK, M], F32, 0), x, 0, slice(0, M))
+        wk_raw1 = placed("wk_raw1", [P, 2, KP], I32, 8192)
+        nc.sync.dma_start(wk_raw1[:], wk_src[:, :, 4 * KP : 8 * KP].bitcast(I32))
+        ts_g = tile("ts_g", [P, J], F32)
+        nc.vector.tensor_copy(ts_g[:], ts_win[:].indirect(offsets[:]))
 
         wk_sc = tile("wk_sc", [P, 2, R], U8)
-        nc.vector.tensor_copy(
-            wk_sc[:].rearrange("p a r -> p (a r)").bitcast(I32).rearrange("p (s t g h) -> p s t g h", t=4, g=16, h=2),
-            wk_sc_raw[:].rearrange("p a r -> p (a r)").bitcast(I32).rearrange("p (s g t h) -> p s t g h", t=4, g=16, h=2),
-        )
-        order_wk(wk_q[1][:].rearrange("p a r -> p (a r)"), wk_raw1[:].rearrange("p a r -> p (a r)"))
+
+        def order_wk_scales():
+            nc.vector.tensor_copy(
+                wk_sc[:].rearrange("p a r -> p (a r)").bitcast(I32).rearrange("p (s t g h) -> p s t g h", t=4, g=16, h=2),
+                wk_sc_raw[:].rearrange("p a r -> p (a r)").bitcast(I32).rearrange("p (s g t h) -> p s t g h", t=4, g=16, h=2),
+            )
 
         v_pair = {}
         v_q = [tile("v_q%d" % h, [P, 2, BANK], U16) for h in range(2)]
@@ -110,20 +132,16 @@ def tile_list_kvt_ts_kernel(
             v_pair[h] = tile("v_pair%d" % h, [P, BANK], U32, "slot3")
             nc.vector.tensor_copy(v_pair[h][:], tab_w[:].indirect(offsets[:, 32 * h : 32 * (h + 1)]))
 
-        def part_words(h):
-            nc.vector.tensor_copy(v_q[h][:], v_pair[h][:].bitcast(U16).rearrange("p (j d) -> p d j", d=2))
+        def part_words(h, j0, j1):
+            nc.vector.tensor_copy(
+                v_q[h][:, :, j0:j1], v_pair[h][:, j0:j1].bitcast(U16).rearrange("p (j d) -> p d j", d=2)
+            )
 
-        def quantize(name, rounded, cols):
-            codes = tile(name + "_q", [P, cols], U32)
+        def quantize(name, rounded, cols, tag=None):
+            codes = tile(name + "_q", [P, cols], U32, tag)
             scales = tile(name + "_s", [P, cols], U8)
             nc.vector.quantize_mx(out=codes[:].bitcast(FP8X4), scales=scales[:], in_=rounded)
             return codes, scales
-
-        def copy_on(engine, out, in_):
-            if engine == "scalar":
-                nc.scalar.copy(out, in_)
-            else:
-                nc.vector.tensor_copy(out, in_)
 
         def round_plain(name, raw, cols, engine, tag=None):
             rounded = tile(name + "_bf", [P, cols * PACK], BF16, tag)
@@ -134,20 +152,18 @@ def tile_list_kvt_ts_kernel(
             )
             return rounded
 
-        def round_wq(a, b, engine, t0=0, t1=4):
-            rounded = tile("wq%d%d%d_bf" % (a, b, t0), [P, (t1 - t0) * P * PACK], BF16)
-            copy_on(
-                engine,
-                rounded[:].rearrange("p (t g u i) -> p t g i u", g=16, u=8, i=PACK),
-                wq_raw[a, b][:].rearrange("p i (g t u) -> p t g i u", t=4, u=8)[:, t0:t1],
-            )
+        def round_wq(a, b, engines):
+            rounded = tile("wq%d%d_bf" % (a, b), [P, KP * PACK], BF16)
+            for h in range(2):
+                copy_on(
+                    engines[h],
+                    rounded[:].rearrange("p (t g h u i) -> p h t g i u", g=16, h=2, u=4, i=PACK)[:, h],
+                    wq_raw[a, b][:].rearrange("p i (g t h u) -> p h t g i u", t=4, h=2, u=4)[:, h],
+                )
             return rounded
 
-        def quantize_wq(a, b, rounded, t0=0, t1=4):
-            codes, scales = quantize("wq%d%d%d" % (a, b, t0), rounded[:], (t1 - t0) * P)
-            for t in range(t0, t1):
-                cols = slice((t - t0) * P, (t - t0 + 1) * P)
-                wq_q[a, b, t] = (codes[:, cols], scales[:, cols])
+        def quantize_wq(a, b, rounded):
+            wq_q[a, b] = quantize("wq%d%d" % (a, b), rounded[:], KP)
 
         kr_bf = {(b, h): tile("kr_bf%d%d" % (b, h), [P, BANK, PACK], BF16) for b in range(2) for h in range(2)}
 
@@ -170,46 +186,44 @@ def tile_list_kvt_ts_kernel(
 
         kr_q = {}
 
-        def quantize_kr(b, h):
-            kr_q[b, h] = quantize("kr%d%d" % (b, h), kr_bf[b, h][:].rearrange("p n t -> p (n t)"), BANK)
+        def quantize_kr(b, h, tag):
+            kr_q[b, h] = quantize("kr%d%d" % (b, h), kr_bf[b, h][:].rearrange("p n t -> p (n t)"), BANK, tag)
 
         x_q = {}
         wq_q = {}
         wq_raw = {}
         half = [slice(0, KP), slice(KP, 2 * KP)]
-        x_raw = tile("x_raw", [P, 2, PACK, M], F32, "slot0")
-        nc.sync.dma_start(x_raw[:].rearrange("p a i c -> p a (i c)"), x.rearrange("(a p i) c -> p a (i c)", a=2, i=PACK))
+        both_vector = ("vector", "vector")
         gather_words(0)
-        part_words(0)
+        order_wk_scales()
+        x_raw1 = load_rows(tile("x_raw1", [P, PACK, M], F32, "slot0"), x, 1, slice(0, M))
+        part_words(0, 0, P)
+        part_words(0, P, BANK)
         gather_words(1)
-        wq_raw[0, 0] = load_rows("wq_raw00", wq, 0, half[0], "slot1")
+        wq_raw[0, 0] = load_rows(tile("wq_raw00", [P, PACK, KP], F32, "slot1"), wq, 0, half[0])
+        part_words(1, 0, BANK)
+        wq_raw[1, 0] = load_rows(tile("wq_raw10", [P, PACK, KP], F32, "slot3"), wq, 1, half[0])
+        order_wk(1, wk_raw1)
         for b in range(2):
-            for c in range(4):
-                kr_bank(b, 0, c)
-        part_words(1)
-        wq_raw[1, 0] = load_rows("wq_raw10", wq, 1, half[0], "slot3")
-        ts_g = tile("ts_g", [P, J], F32)
-        nc.vector.tensor_copy(ts_g[:], ts_win[:].indirect(offsets[:]))
-        wq_raw[0, 1] = load_rows("wq_raw01", wq, 0, half[1], "slot2")
-
-        x_bf0 = round_plain("x0", x_raw[:, 0], M, "vector")
-        x_bf1 = round_plain("x1", x_raw[:, 1], M, "scalar", "slot4")
-        wq_raw[1, 1] = load_rows("wq_raw11", wq, 1, half[1], "slot0")
-        quantize_kr(0, 0)
+            for h in range(2):
+                for c in range(4):
+                    kr_bank(b, h, c)
+        x_bf0 = round_plain("x0", x_raw0[:], M, "vector")
+        wq_raw[0, 1] = load_rows(placed("wq_raw01", [P, PACK, KP], F32, 0), wq, 0, half[1])
+        x_bf1 = round_plain("x1", x_raw1[:], M, "vector")
+        wq_raw[1, 1] = load_rows(tile("wq_raw11", [P, PACK, KP], F32, "slot0"), wq, 1, half[1])
         x_q[0] = quantize("x0", x_bf0[:], M)
-        wq_bf00 = round_wq(0, 0, "vector")
         x_q[1] = quantize("x1", x_bf1[:], M)
-        wv_raw = tile("wv_raw", [P, 2, PACK, N], F32, "slot4")
+        wq_bf00 = round_wq(0, 0, both_vector)
+        wv_raw = tile("wv_raw", [P, 2, PACK, N], F32, "slot1")
         nc.sync.dma_start(wv_raw[:].rearrange("p a i c -> p a (i c)"), wv.rearrange("(a p i) c -> p a (i c)", a=2, i=PACK))
+        quantize_kr(0, 0, "x1_bf")
         quantize_wq(0, 0, wq_bf00)
-        for b in range(2):
-            for c in range(4):
-                kr_bank(b, 1, c)
-        wq_bf10 = round_wq(1, 0, "vector")
-        quantize_kr(1, 0)
+        wq_bf10 = round_wq(1, 0, both_vector)
+        quantize_kr(0, 1, "wq00_bf")
         quantize_wq(1, 0, wq_bf10)
-        wq_bf01 = round_wq(0, 1, "vector")
-        quantize_kr(0, 1)
+        wq_bf01 = round_wq(0, 1, ("scalar", "scalar"))
+        quantize_kr(1, 0, "wq10_bf")
 
         qr_bf = [tile("qr_bf%d" % m, [P, 2, P, PACK], BF16) for m in range(4)]
 
@@ -220,8 +234,8 @@ def tile_list_kvt_ts_kernel(
                 for a in range(2):
                     nc.tensor.matmul_mx(
                         out=acc[:, t, :],
-                        lhsT=wq_q[a, b, t][0].bitcast(FP8X4),
-                        lhsT_scale=wq_q[a, b, t][1],
+                        lhsT=wq_q[a, b][0][:, t * P : (t + 1) * P].bitcast(FP8X4),
+                        lhsT_scale=wq_q[a, b][1][:, t * P : (t + 1) * P],
                         rhs=x_q[a][0][:, cols].bitcast(FP8X4),
                         rhs_scale=x_q[a][1][:, cols],
                         start=(a == 0),
@@ -231,12 +245,10 @@ def tile_list_kvt_ts_kernel(
 
         for m in range(4):
             qr_bank(0, m)
+        wq_bf11 = round_wq(1, 1, both_vector)
         quantize_wq(0, 1, wq_bf01)
-        wq_bf11a = round_wq(1, 1, "vector", 0, 2)
-        wq_bf11b = round_wq(1, 1, "scalar", 2, 4)
-        quantize_kr(1, 1)
-        quantize_wq(1, 1, wq_bf11a, 0, 2)
-        quantize_wq(1, 1, wq_bf11b, 2, 4)
+        quantize_wq(1, 1, wq_bf11)
+        quantize_kr(1, 1, "wq11_bf")
 
         qr_q = {}
 

@@ -28,16 +28,36 @@ def tile_list_kvt_ts_kernel(
     with ExitStack() as ctx:
         sb = ctx.enter_context(tc.tile_pool(name="sb", bufs=1))
         shared = ctx.enter_context(tc.tile_pool(name="shared", bufs=1))
-        psum = ctx.enter_context(tc.psum_pool(name="psum", bufs=8))
+        psum = ctx.enter_context(tc.psum_pool(name="psum", bufs=1))
 
-        def tile(name, shape, dtype, tag=None):
-            return sb.tile(shape, dtype, name=name, tag=tag or name, align_bytes=64)
+        chains = [
+            [("wq_raw10", 8192), ("tab_w", 4 * T), ("ones", 4 * P), ("wv_raw", 8192), ("wq_raw00", 8192)],
+            [("wv0_bf", 2048), ("ts_row", 128), ("wv1_bf", 2048)],
+            [("wk_q0", 4096), ("tab_sc", T), ("wk_sc_raw", 2 * R), ("v_q0", 2048)],
+            [("wq_raw11", 8192), ("wk_raw1", 4096), ("wk_raw0", 4096), ("x_raw0", 8192)],
+            [("x_raw1", 8192), ("ts_win", 4 * T), ("v_pair0", 2048), ("v_pair1", 2048), ("wq_raw01", 8192)],
+            [("kr00_q", 2048), ("wq10_bf", 4096)],
+            [("kr10_q", 2048), ("wq11_bf", 4096), ("kr01_q", 2048)],
+            [("kr11_q", 2048), ("kr_bf01", 4096)],
+        ]
+        where = {}
+        end = 0
+        for chain in chains:
+            for name, size in chain:
+                where[name] = end
+                end = end + size - 64
+            end = end + 64
 
-        def placed(name, shape, dtype, offset):
-            return shared.tile(shape, dtype, name=name, offset=offset, align_bytes=64)
+        def tile(name, shape, dtype):
+            if name in where:
+                return shared.tile(shape, dtype, name=name, offset=where[name], align_bytes=64)
+            return sb.tile(shape, dtype, name=name, align_bytes=64)
+
+        taken = []
 
         def bank(shape):
-            return psum.tile(shape, F32, name="bank")
+            taken.append(len(taken) % 8)
+            return psum.tile(shape, F32, name="bank%d" % len(taken), offset=2048 * taken[-1])
 
         def copy_on(engine, out, in_):
             if engine == "scalar":
@@ -54,15 +74,15 @@ def tile_list_kvt_ts_kernel(
         wk_raw0 = tile("wk_raw0", [P, 2, KP], I32)
         nc.sync.dma_start(wk_raw0[:], wk_src[:, :, 0 : 4 * KP].bitcast(I32))
 
-        tab_sc = placed("tab_sc", [P, T], U8, 6144)
+        tab_sc = tile("tab_sc", [P, T], U8)
         nc.vector.memset(tab_sc[:].bitcast(I32), 0)
         tab_rows = tab_scales.rearrange("a (q r) t -> r q a t", r=4)
         for r in range(4):
             nc.sync.dma_start(tab_sc[r:P:16, :].bitcast(I32), tab_rows[r].bitcast(I32))
 
-        ones = tile("ones", [P, P], F32, "slot1")
+        ones = tile("ones", [P, P], F32)
         ident = tile("ident", [P, P], F32)
-        nc.gpsimd.memset(ones[:], 1.0)
+        nc.vector.memset(ones[:], 1.0)
         nc.gpsimd.affine_select(
             out=ident[:],
             in_=ones[:],
@@ -72,16 +92,12 @@ def tile_list_kvt_ts_kernel(
             base=0,
             channel_multiplier=1,
         )
-        tab_w = tile("tab_w", [P, T], U32, "slot1")
+        wv_raw = tile("wv_raw", [P, 2, PACK, N], F32)
+        nc.sync.dma_start(wv_raw[:].rearrange("p a i c -> p a (i c)"), wv.rearrange("(a p i) c -> p a (i c)", a=2, i=PACK))
+        tab_w = tile("tab_w", [P, T], U32)
         nc.sync.dma_start(tab_w[:].bitcast(I32), tab_words[0].rearrange("p t b -> p (t b)").bitcast(I32))
-
-        wk_sc_raw = tile("wk_sc_raw", [P, 2, R], U8, "slot0")
-        nc.gpsimd.memset(wk_sc_raw[:].rearrange("p a r -> p (a r)").bitcast(I32), 0)
-        wk_rows = wk_scales.rearrange("a (q r) n -> r q a n", r=4)
-        for r in range(4):
-            nc.sync.dma_start(wk_sc_raw[r:P:32, :, :].bitcast(I32), wk_rows[r].bitcast(I32))
         v_sc1 = tile("v_sc1", [P, J], U8)
-        nc.vector.memset(v_sc1[:].bitcast(I32), 0)
+        nc.gpsimd.memset(v_sc1[:].bitcast(I32), 0)
 
         def load_rows(raw, src, a, cols):
             nc.sync.dma_start(raw[:], src[a * KP : (a + 1) * KP, cols].rearrange("(p i) c -> p i c", i=PACK))
@@ -94,7 +110,7 @@ def tile_list_kvt_ts_kernel(
             for c in range(4):
                 col = 4 * g + c
                 nc.tensor.transpose(acc[:, c, :], ts_row[:, col : col + 1].to_broadcast([P, P]), ident[:])
-            copy_on("vector" if g < 2 else "scalar", ts_by_n[:, :, 4 * g : 4 * g + 4], acc[:].rearrange("p c n -> p n c"))
+            copy_on("scalar", ts_by_n[:, :, 4 * g : 4 * g + 4], acc[:].rearrange("p c n -> p n c"))
 
         wk_q = [tile("wk_q%d" % b, [P, 2, KP], I32) for b in range(2)]
 
@@ -104,18 +120,19 @@ def tile_list_kvt_ts_kernel(
                 raw[:].rearrange("p a (g t i) -> p a t g i", t=4, i=8),
             )
 
-        order_wk(0, wk_raw0)
         v_sc0 = tile("v_sc0", [P, J], U8)
-        for h in range(2):
-            cols = slice(h * BANK, (h + 1) * BANK)
-            nc.vector.tensor_copy(v_sc0[:, cols], tab_sc[:].indirect(offsets[:, 32 * h : 32 * (h + 1)]))
-            nc.sync.dma_start(v_sc1[0 : P - 16, cols].bitcast(I32), v_sc0[16:P, cols].bitcast(I32))
+        nc.vector.tensor_copy(v_sc0[:], tab_sc[:].indirect(offsets[:]))
+        nc.sync.dma_start(v_sc1[0 : P - 16, :].bitcast(I32), v_sc0[16:P, :].bitcast(I32))
+        wk_sc_raw = tile("wk_sc_raw", [P, 2, R], U8)
+        nc.vector.memset(wk_sc_raw[:].rearrange("p a r -> p (a r)").bitcast(I32), 0)
+        wk_rows = wk_scales.rearrange("a (q r) n -> r q a n", r=4)
+        for r in range(4):
+            nc.sync.dma_start(wk_sc_raw[r:P:32, :, :].bitcast(I32), wk_rows[r].bitcast(I32))
+        order_wk(0, wk_raw0)
         v_sc = [v_sc0, v_sc1]
-        x_raw0 = load_rows(placed("x_raw0", [P, PACK, M], F32, 0), x, 0, slice(0, M))
-        wk_raw1 = placed("wk_raw1", [P, 2, KP], I32, 8192)
+        wk_raw1 = tile("wk_raw1", [P, 2, KP], I32)
         nc.sync.dma_start(wk_raw1[:], wk_src[:, :, 4 * KP : 8 * KP].bitcast(I32))
-        ts_g = tile("ts_g", [P, J], F32)
-        nc.vector.tensor_copy(ts_g[:], ts_win[:].indirect(offsets[:]))
+        x_raw0 = load_rows(tile("x_raw0", [P, PACK, M], F32), x, 0, slice(0, M))
 
         wk_sc = tile("wk_sc", [P, 2, R], U8)
 
@@ -129,7 +146,7 @@ def tile_list_kvt_ts_kernel(
         v_q = [tile("v_q%d" % h, [P, 2, BANK], U16) for h in range(2)]
 
         def gather_words(h):
-            v_pair[h] = tile("v_pair%d" % h, [P, BANK], U32, "slot3")
+            v_pair[h] = tile("v_pair%d" % h, [P, BANK], U32)
             nc.vector.tensor_copy(v_pair[h][:], tab_w[:].indirect(offsets[:, 32 * h : 32 * (h + 1)]))
 
         def part_words(h, j0, j1):
@@ -137,14 +154,14 @@ def tile_list_kvt_ts_kernel(
                 v_q[h][:, :, j0:j1], v_pair[h][:, j0:j1].bitcast(U16).rearrange("p (j d) -> p d j", d=2)
             )
 
-        def quantize(name, rounded, cols, tag=None):
-            codes = tile(name + "_q", [P, cols], U32, tag)
+        def quantize(name, rounded, cols):
+            codes = tile(name + "_q", [P, cols], U32)
             scales = tile(name + "_s", [P, cols], U8)
             nc.vector.quantize_mx(out=codes[:].bitcast(FP8X4), scales=scales[:], in_=rounded)
             return codes, scales
 
-        def round_plain(name, raw, cols, engine, tag=None):
-            rounded = tile(name + "_bf", [P, cols * PACK], BF16, tag)
+        def round_plain(name, raw, cols, engine):
+            rounded = tile(name + "_bf", [P, cols * PACK], BF16)
             copy_on(
                 engine,
                 rounded[:].rearrange("p (c u i) -> p c i u", u=4, i=PACK),
@@ -186,46 +203,53 @@ def tile_list_kvt_ts_kernel(
 
         kr_q = {}
 
-        def quantize_kr(b, h, tag):
-            kr_q[b, h] = quantize("kr%d%d" % (b, h), kr_bf[b, h][:].rearrange("p n t -> p (n t)"), BANK, tag)
+        def quantize_kr(b, h):
+            kr_q[b, h] = quantize("kr%d%d" % (b, h), kr_bf[b, h][:].rearrange("p n t -> p (n t)"), BANK)
 
         x_q = {}
         wq_q = {}
         wq_raw = {}
         half = [slice(0, KP), slice(KP, 2 * KP)]
         both_vector = ("vector", "vector")
+        wv_q = {}
+        ts_g = tile("ts_g", [P, J], F32)
+        nc.vector.tensor_copy(ts_g[:], ts_win[:].indirect(offsets[:]))
+        x_raw1 = load_rows(tile("x_raw1", [P, PACK, M], F32), x, 1, slice(0, M))
+        wv_bf0 = round_plain("wv0", wv_raw[:, 0], N, "scalar")
+        wv_bf1 = round_plain("wv1", wv_raw[:, 1], N, "scalar")
+        wq_raw[0, 0] = load_rows(tile("wq_raw00", [P, PACK, KP], F32), wq, 0, half[0])
         gather_words(0)
         order_wk_scales()
-        x_raw1 = load_rows(tile("x_raw1", [P, PACK, M], F32, "slot0"), x, 1, slice(0, M))
         part_words(0, 0, P)
         part_words(0, P, BANK)
+        wv_q[0] = quantize("wv0", wv_bf0[:], N)
+        wv_q[1] = quantize("wv1", wv_bf1[:], N)
         gather_words(1)
-        wq_raw[0, 0] = load_rows(tile("wq_raw00", [P, PACK, KP], F32, "slot1"), wq, 0, half[0])
+        wq_raw[1, 0] = load_rows(tile("wq_raw10", [P, PACK, KP], F32), wq, 1, half[0])
         part_words(1, 0, BANK)
-        wq_raw[1, 0] = load_rows(tile("wq_raw10", [P, PACK, KP], F32, "slot3"), wq, 1, half[0])
+        wq_raw[0, 1] = load_rows(tile("wq_raw01", [P, PACK, KP], F32), wq, 0, half[1])
         order_wk(1, wk_raw1)
+        wq_raw[1, 1] = load_rows(tile("wq_raw11", [P, PACK, KP], F32), wq, 1, half[1])
         for b in range(2):
             for h in range(2):
                 for c in range(4):
                     kr_bank(b, h, c)
         x_bf0 = round_plain("x0", x_raw0[:], M, "vector")
-        wq_raw[0, 1] = load_rows(placed("wq_raw01", [P, PACK, KP], F32, 0), wq, 0, half[1])
         x_bf1 = round_plain("x1", x_raw1[:], M, "vector")
-        wq_raw[1, 1] = load_rows(tile("wq_raw11", [P, PACK, KP], F32, "slot0"), wq, 1, half[1])
         x_q[0] = quantize("x0", x_bf0[:], M)
-        x_q[1] = quantize("x1", x_bf1[:], M)
         wq_bf00 = round_wq(0, 0, both_vector)
-        wv_raw = tile("wv_raw", [P, 2, PACK, N], F32, "slot1")
-        nc.sync.dma_start(wv_raw[:].rearrange("p a i c -> p a (i c)"), wv.rearrange("(a p i) c -> p a (i c)", a=2, i=PACK))
-        quantize_kr(0, 0, "x1_bf")
+        x_q[1] = quantize("x1", x_bf1[:], M)
         quantize_wq(0, 0, wq_bf00)
         wq_bf10 = round_wq(1, 0, both_vector)
-        quantize_kr(0, 1, "wq00_bf")
         quantize_wq(1, 0, wq_bf10)
-        wq_bf01 = round_wq(0, 1, ("scalar", "scalar"))
-        quantize_kr(1, 0, "wq10_bf")
+        wq_bf01 = round_wq(0, 1, both_vector)
+        quantize_kr(0, 0)
+        quantize_wq(0, 1, wq_bf01)
+        wq_bf11 = round_wq(1, 1, both_vector)
+        quantize_wq(1, 1, wq_bf11)
+        quantize_kr(1, 0)
 
-        qr_bf = [tile("qr_bf%d" % m, [P, 2, P, PACK], BF16) for m in range(4)]
+        qr_bf = tile("qr_bf", [P, 4, 2, P, PACK], BF16)
 
         def qr_bank(b, m):
             acc = bank([P, 4, P])
@@ -241,76 +265,64 @@ def tile_list_kvt_ts_kernel(
                         start=(a == 0),
                         stop=(a == 1),
                     )
-            nc.scalar.copy(qr_bf[m][:, b, :, :], acc[:].rearrange("p t n -> p n t"))
+            nc.scalar.copy(qr_bf[:, m, b, :, :], acc[:].rearrange("p t n -> p n t"))
 
         for m in range(4):
             qr_bank(0, m)
-        wq_bf11 = round_wq(1, 1, both_vector)
-        quantize_wq(0, 1, wq_bf01)
-        quantize_wq(1, 1, wq_bf11)
-        quantize_kr(1, 1, "wq11_bf")
 
         qr_q = {}
 
         def quantize_qr(m):
-            qr_q[m] = quantize("qr%d" % m, qr_bf[m][:].rearrange("p b n t -> p (b n t)"), 2 * P)
+            qr_q[m] = quantize("qr%d" % m, qr_bf[:, m].rearrange("p b n t -> p (b n t)"), 2 * P)
 
-        def scores(m):
-            res = tile("sc%d" % m, [P, J], F32)
+        def scores(m, h):
+            res = tile("sc%d%d" % (m, h), [P, BANK], F32)
+            acc = bank([P, BANK])
+            for b in range(2):
+                nc.tensor.matmul_mx(
+                    out=acc[:],
+                    lhsT=qr_q[m][0][:, b * P : (b + 1) * P].bitcast(FP8X4),
+                    lhsT_scale=qr_q[m][1][:, b * P : (b + 1) * P],
+                    rhs=kr_q[b, h][0][:].bitcast(FP8X4),
+                    rhs_scale=kr_q[b, h][1][:],
+                    start=(b == 0),
+                    stop=(b == 1),
+                )
+            nc.vector.tensor_tensor(res[:], acc[:], ts_g[:, h * BANK : (h + 1) * BANK], MULT)
+            nc.sync.dma_start(out_0[m * P : (m + 1) * P, h * BANK : (h + 1) * BANK], res[:])
+
+        def values(n, h):
+            res = tile("vv%d%d" % (n, h), [P, BANK], F32)
+            acc = bank([P, BANK])
+            cols = slice(h * BANK, (h + 1) * BANK)
+            for a in range(2):
+                nc.tensor.matmul_mx(
+                    out=acc[:],
+                    lhsT=wv_q[a][0][:, n * P : (n + 1) * P].bitcast(FP8X4),
+                    lhsT_scale=wv_q[a][1][:, n * P : (n + 1) * P],
+                    rhs=v_q[h][:, a, :].bitcast(FP4X4),
+                    rhs_scale=v_sc[a][:, cols],
+                    start=(a == 0),
+                    stop=(a == 1),
+                )
+            nc.scalar.copy(res[:], acc[:])
+            nc.sync.dma_start(out_1[n * P : (n + 1) * P, cols], res[:])
+
+        for n in range(2):
             for h in range(2):
-                acc = bank([P, BANK])
-                for b in range(2):
-                    nc.tensor.matmul_mx(
-                        out=acc[:],
-                        lhsT=qr_q[m][0][:, b * P : (b + 1) * P].bitcast(FP8X4),
-                        lhsT_scale=qr_q[m][1][:, b * P : (b + 1) * P],
-                        rhs=kr_q[b, h][0][:].bitcast(FP8X4),
-                        rhs_scale=kr_q[b, h][1][:],
-                        start=(b == 0),
-                        stop=(b == 1),
-                    )
-                cols = slice(h * BANK, (h + 1) * BANK)
-                nc.vector.tensor_tensor(res[:, cols], acc[:], ts_g[:, cols], MULT)
-                if m == 3:
-                    nc.sync.dma_start(out_0[m * P : (m + 1) * P, cols], res[:, cols])
-            if m < 3:
-                nc.sync.dma_start(out_0[m * P : (m + 1) * P, :], res[:])
-
-        wv_q = {}
-
-        def values(n):
-            res = tile("vv%d" % n, [P, J], F32)
-            for h in range(2):
-                acc = bank([P, BANK])
-                cols = slice(h * BANK, (h + 1) * BANK)
-                for a in range(2):
-                    nc.tensor.matmul_mx(
-                        out=acc[:],
-                        lhsT=wv_q[a][0][:, n * P : (n + 1) * P].bitcast(FP8X4),
-                        lhsT_scale=wv_q[a][1][:, n * P : (n + 1) * P],
-                        rhs=v_q[h][:, a, :].bitcast(FP4X4),
-                        rhs_scale=v_sc[a][:, cols],
-                        start=(a == 0),
-                        stop=(a == 1),
-                    )
-                nc.scalar.copy(res[:, cols], acc[:])
-            nc.sync.dma_start(out_1[n * P : (n + 1) * P, :], res[:])
-
-        qr_bank(1, 0)
-        qr_bank(1, 1)
+                values(n, h)
+        for m in range(4):
+            qr_bank(1, m)
+        quantize_kr(0, 1)
         quantize_qr(0)
-        wv_bf0 = round_plain("wv0", wv_raw[:, 0], N, "scalar")
-        qr_bank(1, 2)
         quantize_qr(1)
-        scores(0)
-        qr_bank(1, 3)
-        wv_bf1 = round_plain("wv1", wv_raw[:, 1], N, "scalar")
-        wv_q[0] = quantize("wv0", wv_bf0[:], N)
+        scores(0, 0)
+        quantize_kr(1, 1)
+        scores(1, 0)
         quantize_qr(2)
-        scores(1)
-        wv_q[1] = quantize("wv1", wv_bf1[:], N)
+        scores(0, 1)
         quantize_qr(3)
-        values(0)
-        scores(2)
-        values(1)
-        scores(3)
+        scores(1, 1)
+        for m in range(2, 4):
+            for h in range(2):
+                scores(m, h)

@@ -31,14 +31,13 @@ def tile_list_kvt_ts_kernel(
         psum = ctx.enter_context(tc.psum_pool(name="psum", bufs=1))
 
         chains = [
-            [("wq_raw10", 8192), ("tab_w", 4 * T), ("ones", 4 * P), ("wv_raw", 8192), ("wq_raw00", 8192)],
-            [("wv0_bf", 2048), ("ts_row", 128), ("wv1_bf", 2048)],
-            [("wk_q0", 4096), ("tab_sc", T), ("wk_sc_raw", 2 * R), ("v_q0", 2048)],
-            [("wq_raw11", 8192), ("wk_raw1", 4096), ("wk_raw0", 4096), ("x_raw0", 8192)],
-            [("x_raw1", 8192), ("ts_win", 4 * T), ("v_pair0", 2048), ("v_pair1", 2048), ("wq_raw01", 8192)],
-            [("kr00_q", 2048), ("wq10_bf", 4096)],
-            [("kr10_q", 2048), ("wq11_bf", 4096), ("kr01_q", 2048)],
+            [("wq_raw10", 8192), ("tab_w", 4 * T), ("zeros", 2 * R), ("wv_raw0", 4096)],
             [("kr11_q", 2048), ("kr_bf01", 4096)],
+            [("wk_sc_raw", 2 * R), ("v_q0", 2048)],
+            [("kr_bf00", 4096), ("wv_raw1", 4096), ("tab_sc", T), ("x_raw0", 8192), ("wq_raw11", 8192)],
+            [("x_raw1", 8192), ("ts_win", 4 * T), ("v_pair0", 2048), ("v_pair1", 2048), ("wq_raw01", 8192)],
+            [("kr00_q", 2048), ("wq01_bf", 4096)],
+            [("kr10_q", 2048), ("wq11_bf", 4096), ("kr01_q", 2048)],
         ]
         where = {}
         end = 0
@@ -47,6 +46,7 @@ def tile_list_kvt_ts_kernel(
                 where[name] = end
                 end = end + size - 64
             end = end + 64
+        where["wq_raw00"] = where["ts_win"] + 64
 
         def tile(name, shape, dtype):
             if name in where:
@@ -69,10 +69,9 @@ def tile_list_kvt_ts_kernel(
         nc.sync.dma_start(offsets[:], offs)
 
         ts_row = tile("ts_row", [P, T // P], F32)
-        nc.scalar.dma_start(ts_row[:], ts[0, :].rearrange("(n c) -> n c", n=P))
-        wk_src = wk_words.rearrange("a p r i -> p a (r i)")
-        wk_raw0 = tile("wk_raw0", [P, 2, KP], I32)
-        nc.sync.dma_start(wk_raw0[:], wk_src[:, :, 0 : 4 * KP].bitcast(I32))
+        nc.sync.dma_start(ts_row[:], ts[0, :].rearrange("(n c) -> n c", n=P))
+        wk_raw = tile("wk_raw", [P, 2, R], I32)
+        nc.sync.dma_start(wk_raw[:], wk_words.rearrange("a p r i -> p a (r i)").bitcast(I32))
 
         tab_sc = tile("tab_sc", [P, T], U8)
         nc.vector.memset(tab_sc[:].bitcast(I32), 0)
@@ -92,12 +91,17 @@ def tile_list_kvt_ts_kernel(
             base=0,
             channel_multiplier=1,
         )
-        wv_raw = tile("wv_raw", [P, 2, PACK, N], F32)
-        nc.sync.dma_start(wv_raw[:].rearrange("p a i c -> p a (i c)"), wv.rearrange("(a p i) c -> p a (i c)", a=2, i=PACK))
+        zeros = tile("zeros", [P, 2 * R // 4], I32)
+        nc.vector.memset(zeros[:], 0)
+        v_sc1 = tile("v_sc1", [P, J], U8)
+        nc.vector.memset(v_sc1[:].bitcast(I32), 0)
+        wk_sc_raw = tile("wk_sc_raw", [P, 2, R], U8)
+        nc.vector.tensor_copy(wk_sc_raw[:].rearrange("p a r -> p (a r)").bitcast(I32), zeros[:])
         tab_w = tile("tab_w", [P, T], U32)
         nc.sync.dma_start(tab_w[:].bitcast(I32), tab_words[0].rearrange("p t b -> p (t b)").bitcast(I32))
-        v_sc1 = tile("v_sc1", [P, J], U8)
-        nc.gpsimd.memset(v_sc1[:].bitcast(I32), 0)
+        wk_rows = wk_scales.rearrange("a (q r) n -> r q a n", r=4)
+        for r in range(4):
+            nc.sync.dma_start(wk_sc_raw[r:P:32, :, :].bitcast(I32), wk_rows[r].bitcast(I32))
 
         def load_rows(raw, src, a, cols):
             nc.sync.dma_start(raw[:], src[a * KP : (a + 1) * KP, cols].rearrange("(p i) c -> p i c", i=PACK))
@@ -112,26 +116,17 @@ def tile_list_kvt_ts_kernel(
                 nc.tensor.transpose(acc[:, c, :], ts_row[:, col : col + 1].to_broadcast([P, P]), ident[:])
             copy_on("scalar", ts_by_n[:, :, 4 * g : 4 * g + 4], acc[:].rearrange("p c n -> p n c"))
 
-        wk_q = [tile("wk_q%d" % b, [P, 2, KP], I32) for b in range(2)]
-
-        def order_wk(b, raw):
-            nc.vector.tensor_copy(
-                wk_q[b][:].rearrange("p a (t g i) -> p a t g i", t=4, i=8),
-                raw[:].rearrange("p a (g t i) -> p a t g i", t=4, i=8),
-            )
-
+        wv_raw0 = load_rows(tile("wv_raw0", [P, PACK, N], F32), wv, 0, slice(0, N))
+        wk_q = tile("wk_q", [P, 2, R], I32)
+        nc.vector.tensor_copy(
+            wk_q[:].rearrange("p a (b t g i) -> p (a b) t g i", b=2, t=4, i=8),
+            wk_raw[:].rearrange("p a (b g t i) -> p (a b) t g i", b=2, t=4, i=8),
+        )
         v_sc0 = tile("v_sc0", [P, J], U8)
         nc.vector.tensor_copy(v_sc0[:], tab_sc[:].indirect(offsets[:]))
         nc.sync.dma_start(v_sc1[0 : P - 16, :].bitcast(I32), v_sc0[16:P, :].bitcast(I32))
-        wk_sc_raw = tile("wk_sc_raw", [P, 2, R], U8)
-        nc.vector.memset(wk_sc_raw[:].rearrange("p a r -> p (a r)").bitcast(I32), 0)
-        wk_rows = wk_scales.rearrange("a (q r) n -> r q a n", r=4)
-        for r in range(4):
-            nc.sync.dma_start(wk_sc_raw[r:P:32, :, :].bitcast(I32), wk_rows[r].bitcast(I32))
-        order_wk(0, wk_raw0)
         v_sc = [v_sc0, v_sc1]
-        wk_raw1 = tile("wk_raw1", [P, 2, KP], I32)
-        nc.sync.dma_start(wk_raw1[:], wk_src[:, :, 4 * KP : 8 * KP].bitcast(I32))
+        wv_raw = [wv_raw0, load_rows(tile("wv_raw1", [P, PACK, N], F32), wv, 1, slice(0, N))]
         x_raw0 = load_rows(tile("x_raw0", [P, PACK, M], F32), x, 0, slice(0, M))
 
         wk_sc = tile("wk_sc", [P, 2, R], U8)
@@ -192,7 +187,7 @@ def tile_list_kvt_ts_kernel(
                 for a in range(2):
                     nc.tensor.matmul_mx(
                         out=acc[:, t, :],
-                        lhsT=wk_q[b][:, a, t * P : (t + 1) * P].bitcast(FP8X4),
+                        lhsT=wk_q[:, a, b * KP + t * P : b * KP + (t + 1) * P].bitcast(FP8X4),
                         lhsT_scale=wk_sc[:, a, b * KP + t * P : b * KP + (t + 1) * P],
                         rhs=v_q[h][:, a, cols].bitcast(FP4X4),
                         rhs_scale=v_sc[a][:, jcols],
@@ -215,26 +210,25 @@ def tile_list_kvt_ts_kernel(
         ts_g = tile("ts_g", [P, J], F32)
         nc.vector.tensor_copy(ts_g[:], ts_win[:].indirect(offsets[:]))
         x_raw1 = load_rows(tile("x_raw1", [P, PACK, M], F32), x, 1, slice(0, M))
-        wv_bf0 = round_plain("wv0", wv_raw[:, 0], N, "scalar")
-        wv_bf1 = round_plain("wv1", wv_raw[:, 1], N, "scalar")
         wq_raw[0, 0] = load_rows(tile("wq_raw00", [P, PACK, KP], F32), wq, 0, half[0])
+        wv_bf0 = round_plain("wv0", wv_raw[0][:], N, "scalar")
+        wv_bf1 = round_plain("wv1", wv_raw[1][:], N, "scalar")
         gather_words(0)
         order_wk_scales()
         part_words(0, 0, P)
         part_words(0, P, BANK)
-        wv_q[0] = quantize("wv0", wv_bf0[:], N)
-        wv_q[1] = quantize("wv1", wv_bf1[:], N)
         gather_words(1)
         wq_raw[1, 0] = load_rows(tile("wq_raw10", [P, PACK, KP], F32), wq, 1, half[0])
         part_words(1, 0, BANK)
         wq_raw[0, 1] = load_rows(tile("wq_raw01", [P, PACK, KP], F32), wq, 0, half[1])
-        order_wk(1, wk_raw1)
-        wq_raw[1, 1] = load_rows(tile("wq_raw11", [P, PACK, KP], F32), wq, 1, half[1])
+        wv_q[0] = quantize("wv0", wv_bf0[:], N)
+        wv_q[1] = quantize("wv1", wv_bf1[:], N)
         for b in range(2):
             for h in range(2):
                 for c in range(4):
                     kr_bank(b, h, c)
         x_bf0 = round_plain("x0", x_raw0[:], M, "vector")
+        wq_raw[1, 1] = load_rows(tile("wq_raw11", [P, PACK, KP], F32), wq, 1, half[1])
         x_bf1 = round_plain("x1", x_raw1[:], M, "vector")
         x_q[0] = quantize("x0", x_bf0[:], M)
         wq_bf00 = round_wq(0, 0, both_vector)
@@ -243,32 +237,29 @@ def tile_list_kvt_ts_kernel(
         wq_bf10 = round_wq(1, 0, both_vector)
         quantize_wq(1, 0, wq_bf10)
         wq_bf01 = round_wq(0, 1, both_vector)
-        quantize_kr(0, 0)
         quantize_wq(0, 1, wq_bf01)
         wq_bf11 = round_wq(1, 1, both_vector)
+        quantize_kr(0, 0)
         quantize_wq(1, 1, wq_bf11)
         quantize_kr(1, 0)
 
         qr_bf = tile("qr_bf", [P, 4, 2, P, PACK], BF16)
 
-        def qr_bank(b, m):
-            acc = bank([P, 4, P])
+        def qr_pass(acc, a, b, m):
             cols = slice(m * P, (m + 1) * P)
             for t in range(4):
-                for a in range(2):
-                    nc.tensor.matmul_mx(
-                        out=acc[:, t, :],
-                        lhsT=wq_q[a, b][0][:, t * P : (t + 1) * P].bitcast(FP8X4),
-                        lhsT_scale=wq_q[a, b][1][:, t * P : (t + 1) * P],
-                        rhs=x_q[a][0][:, cols].bitcast(FP8X4),
-                        rhs_scale=x_q[a][1][:, cols],
-                        start=(a == 0),
-                        stop=(a == 1),
-                    )
-            nc.scalar.copy(qr_bf[:, m, b, :, :], acc[:].rearrange("p t n -> p n t"))
+                nc.tensor.matmul_mx(
+                    out=acc[:, t, :],
+                    lhsT=wq_q[a, b][0][:, t * P : (t + 1) * P].bitcast(FP8X4),
+                    lhsT_scale=wq_q[a, b][1][:, t * P : (t + 1) * P],
+                    rhs=x_q[a][0][:, cols].bitcast(FP8X4),
+                    rhs_scale=x_q[a][1][:, cols],
+                    start=(a == 0 and t == 0),
+                    stop=(a == 1 and t == 3),
+                )
 
-        for m in range(4):
-            qr_bank(0, m)
+        def qr_out(acc, b, m):
+            nc.scalar.copy(qr_bf[:, m, b, :, :], acc[:].rearrange("p t n -> p n t"))
 
         qr_q = {}
 
@@ -312,7 +303,16 @@ def tile_list_kvt_ts_kernel(
             for h in range(2):
                 values(n, h)
         for m in range(4):
-            qr_bank(1, m)
+            acc = bank([P, 4, P])
+            qr_pass(acc, 0, 0, m)
+            qr_pass(acc, 1, 0, m)
+            qr_out(acc, 0, m)
+        accs = [bank([P, 4, P]) for m in range(4)]
+        for m in range(4):
+            qr_pass(accs[m], 0, 1, m)
+        for m in range(4):
+            qr_pass(accs[m], 1, 1, m)
+            qr_out(accs[m], 1, m)
         quantize_kr(0, 1)
         quantize_qr(0)
         quantize_qr(1)

@@ -31,10 +31,11 @@ def tile_list_kvt_ts_kernel(
         psum = ctx.enter_context(tc.psum_pool(name="psum", bufs=1))
 
         chains = [
-            [("wq_raw10", 8192), ("tab_w", 4 * T), ("zeros", 2 * R), ("wv_raw0", 4096)],
+            [("wq_raw10", 8192), ("tab_w", 4 * T), ("zeros", 2 * R), ("wk_raw1", 4096), ("x_raw0", 8192), ("wq_raw11", 8192)],
+            [("wk_raw0", 4096), ("wv_raw0", 4096)],
             [("kr11_q", 2048), ("kr_bf01", 4096)],
             [("wk_sc_raw", 2 * R), ("v_q0", 2048)],
-            [("kr_bf00", 4096), ("wv_raw1", 4096), ("tab_sc", T), ("x_raw0", 8192), ("wq_raw11", 8192)],
+            [("kr_bf00", 4096), ("wv_raw1", 4096), ("tab_sc", T), ("wk_q1", 4096)],
             [("x_raw1", 8192), ("ts_win", 4 * T), ("v_pair0", 2048), ("v_pair1", 2048), ("wq_raw01", 8192)],
             [("kr00_q", 2048), ("wq01_bf", 4096)],
             [("kr10_q", 2048), ("wq11_bf", 4096), ("kr01_q", 2048)],
@@ -70,8 +71,8 @@ def tile_list_kvt_ts_kernel(
 
         ts_row = tile("ts_row", [P, T // P], F32)
         nc.sync.dma_start(ts_row[:], ts[0, :].rearrange("(n c) -> n c", n=P))
-        wk_raw = tile("wk_raw", [P, 2, R], I32)
-        nc.sync.dma_start(wk_raw[:], wk_words.rearrange("a p r i -> p a (r i)").bitcast(I32))
+        wk_raw0 = tile("wk_raw0", [P, R], I32)
+        nc.sync.dma_start(wk_raw0[:], wk_words[0].rearrange("p r i -> p (r i)").bitcast(I32))
 
         tab_sc = tile("tab_sc", [P, T], U8)
         nc.vector.memset(tab_sc[:].bitcast(I32), 0)
@@ -97,6 +98,8 @@ def tile_list_kvt_ts_kernel(
         nc.vector.memset(v_sc1[:].bitcast(I32), 0)
         wk_sc_raw = tile("wk_sc_raw", [P, 2, R], U8)
         nc.vector.tensor_copy(wk_sc_raw[:].rearrange("p a r -> p (a r)").bitcast(I32), zeros[:])
+        wk_raw1 = tile("wk_raw1", [P, R], I32)
+        nc.sync.dma_start(wk_raw1[:], wk_words[1].rearrange("p r i -> p (r i)").bitcast(I32))
         tab_w = tile("tab_w", [P, T], U32)
         nc.sync.dma_start(tab_w[:].bitcast(I32), tab_words[0].rearrange("p t b -> p (t b)").bitcast(I32))
         wk_rows = wk_scales.rearrange("a (q r) n -> r q a n", r=4)
@@ -116,17 +119,23 @@ def tile_list_kvt_ts_kernel(
                 nc.tensor.transpose(acc[:, c, :], ts_row[:, col : col + 1].to_broadcast([P, P]), ident[:])
             copy_on("scalar", ts_by_n[:, :, 4 * g : 4 * g + 4], acc[:].rearrange("p c n -> p n c"))
 
+        wk_q = {}
+
+        def order_wk(a, raw):
+            wk_q[a] = tile("wk_q%d" % a, [P, R], I32)
+            nc.vector.tensor_copy(
+                wk_q[a][:].rearrange("p (b t g i) -> p b t g i", b=2, t=4, i=8),
+                raw[:].rearrange("p (b g t i) -> p b t g i", b=2, t=4, i=8),
+            )
+
+        order_wk(0, wk_raw0)
         wv_raw0 = load_rows(tile("wv_raw0", [P, PACK, N], F32), wv, 0, slice(0, N))
-        wk_q = tile("wk_q", [P, 2, R], I32)
-        nc.vector.tensor_copy(
-            wk_q[:].rearrange("p a (b t g i) -> p (a b) t g i", b=2, t=4, i=8),
-            wk_raw[:].rearrange("p a (b g t i) -> p (a b) t g i", b=2, t=4, i=8),
-        )
         v_sc0 = tile("v_sc0", [P, J], U8)
         nc.vector.tensor_copy(v_sc0[:], tab_sc[:].indirect(offsets[:]))
         nc.sync.dma_start(v_sc1[0 : P - 16, :].bitcast(I32), v_sc0[16:P, :].bitcast(I32))
         v_sc = [v_sc0, v_sc1]
         wv_raw = [wv_raw0, load_rows(tile("wv_raw1", [P, PACK, N], F32), wv, 1, slice(0, N))]
+        order_wk(1, wk_raw1)
         x_raw0 = load_rows(tile("x_raw0", [P, PACK, M], F32), x, 0, slice(0, M))
 
         wk_sc = tile("wk_sc", [P, 2, R], U8)
@@ -187,7 +196,7 @@ def tile_list_kvt_ts_kernel(
                 for a in range(2):
                     nc.tensor.matmul_mx(
                         out=acc[:, t, :],
-                        lhsT=wk_q[:, a, b * KP + t * P : b * KP + (t + 1) * P].bitcast(FP8X4),
+                        lhsT=wk_q[a][:, b * KP + t * P : b * KP + (t + 1) * P].bitcast(FP8X4),
                         lhsT_scale=wk_sc[:, a, b * KP + t * P : b * KP + (t + 1) * P],
                         rhs=v_q[h][:, a, cols].bitcast(FP4X4),
                         rhs_scale=v_sc[a][:, jcols],

@@ -19,6 +19,7 @@ P = 128
 PACK = 4
 KP = P * PACK
 BANK = 512
+LAP = 64
 
 
 def tile_list_kvt_ts_kernel(
@@ -31,23 +32,42 @@ def tile_list_kvt_ts_kernel(
         psum = ctx.enter_context(tc.psum_pool(name="psum", bufs=1))
 
         chains = [
-            [("wq_raw10", 8192), ("tab_w", 4 * T), ("zeros", 2 * R), ("wk_raw1", 4096), ("x_raw0", 8192), ("wq_raw11", 8192)],
-            [("wk_raw0", 4096), ("wv_raw0", 4096)],
-            [("kr11_q", 2048), ("kr_bf01", 4096)],
-            [("wk_sc_raw", 2 * R), ("v_q0", 2048)],
-            [("kr_bf00", 4096), ("wv_raw1", 4096), ("tab_sc", T), ("wk_q1", 4096)],
-            [("x_raw1", 8192), ("ts_win", 4 * T), ("v_pair0", 2048), ("v_pair1", 2048), ("wq_raw01", 8192)],
-            [("kr00_q", 2048), ("wq01_bf", 4096)],
-            [("kr10_q", 2048), ("wq11_bf", 4096), ("kr01_q", 2048)],
+            [("ts_g", 4096), ("wk_raw", 8192), ("room", 4096)],
+            [("x_raw0", 8192), ("sc_rows", J), ("x_raw1", 8192)],
+            [("wq_raw00", 8192), ("both_rows", J + R), ("wq_raw10", 8192)],
+            [("wq_raw01", 8192), ("v_pair0", 2048)],
+            [("wq_raw11", 8192), ("tab_w", 4 * T), ("wv_raw1", 4096)],
+            [("wq10_q", 2048), ("wv_bf", 4096)],
+            [("kr_bf00", 4096)],
+            [("kr_bf10", 4096)],
+            [("kr_bf01", 4096)],
         ]
         where = {}
         end = 0
         for chain in chains:
             for name, size in chain:
                 where[name] = end
-                end = end + size - 64
-            end = end + 64
-        where["wq_raw00"] = where["ts_win"] + 64
+                end = end + size - LAP
+            end = end + LAP
+        where["v_pair1"] = where["wk_raw"] + 4096
+        where["x1_bf"] = where["v_pair1"] + 2048 - LAP
+        where["wv_raw0"] = where["tab_w"] + LAP
+        where["x0_bf"] = where["wv_raw0"] + 4096
+        where["wq00_bf"] = where["wk_raw"] + LAP
+        where["qr0_q"] = where["kr_bf10"] + 2048
+        where["kr11_q"] = where["wq_raw11"] + 4096
+        for later, earlier in [
+            ("wk_rows", "sc_rows"),
+            ("wq10_bf", "x1_bf"),
+            ("x0_q", "wq00_bf"),
+            ("wq01_bf", "x0_bf"),
+            ("kr00_q", "wq10_bf"),
+            ("wq11_bf", "kr_bf00"),
+            ("kr10_q", "wq01_bf"),
+            ("wv_q", "kr_bf10"),
+            ("kr01_q", "wq_raw11"),
+        ]:
+            where[later] = where[earlier]
 
         def tile(name, shape, dtype):
             if name in where:
@@ -60,25 +80,19 @@ def tile_list_kvt_ts_kernel(
             taken.append(len(taken) % 8)
             return psum.tile(shape, F32, name="bank%d" % len(taken), offset=2048 * taken[-1])
 
-        def copy_on(engine, out, in_):
-            if engine == "scalar":
-                nc.scalar.copy(out, in_)
-            else:
-                nc.vector.tensor_copy(out, in_)
-
-        offsets = tile("offsets", [P, J // 16], U16)
-        nc.sync.dma_start(offsets[:], offs)
-
         ts_row = tile("ts_row", [P, T // P], F32)
         nc.sync.dma_start(ts_row[:], ts[0, :].rearrange("(n c) -> n c", n=P))
-        wk_raw0 = tile("wk_raw0", [P, R], I32)
-        nc.sync.dma_start(wk_raw0[:], wk_words[0].rearrange("p r i -> p (r i)").bitcast(I32))
-
+        offsets = tile("offsets", [P, J // 16], U16)
+        nc.sync.dma_start(offsets[:], offs)
         tab_sc = tile("tab_sc", [P, T], U8)
-        nc.vector.memset(tab_sc[:].bitcast(I32), 0)
-        tab_rows = tab_scales.rearrange("a (q r) t -> r q a t", r=4)
-        for r in range(4):
-            nc.sync.dma_start(tab_sc[r:P:16, :].bitcast(I32), tab_rows[r].bitcast(I32))
+        nc.sync.dma_start(tab_sc[96:P, :].bitcast(I32), tab_scales.rearrange("a q t -> q a t").bitcast(I32))
+        wk_rows = tile("wk_rows", [P, R], U8)
+        nc.sync.dma_start(wk_rows[96:P, :].bitcast(I32), wk_scales.rearrange("a q r -> q a r").bitcast(I32))
+        tab_w = tile("tab_w", [P, T], U32)
+        nc.sync.dma_start(tab_w[:].bitcast(I32), tab_words[0].rearrange("p t b -> p (t b)").bitcast(I32))
+        wk_raw = tile("wk_raw", [P, 2, R], I32)
+        for a in range(2):
+            nc.sync.dma_start(wk_raw[:, a, :], wk_words[a].rearrange("p r i -> p (r i)").bitcast(I32))
 
         ones = tile("ones", [P, P], F32)
         ident = tile("ident", [P, P], F32)
@@ -92,21 +106,12 @@ def tile_list_kvt_ts_kernel(
             base=0,
             channel_multiplier=1,
         )
-        zeros = tile("zeros", [P, 2 * R // 4], I32)
-        nc.vector.memset(zeros[:], 0)
-        v_sc1 = tile("v_sc1", [P, J], U8)
-        nc.vector.memset(v_sc1[:].bitcast(I32), 0)
-        wk_sc_raw = tile("wk_sc_raw", [P, 2, R], U8)
-        nc.vector.tensor_copy(wk_sc_raw[:].rearrange("p a r -> p (a r)").bitcast(I32), zeros[:])
-        wk_raw1 = tile("wk_raw1", [P, R], I32)
-        nc.sync.dma_start(wk_raw1[:], wk_words[1].rearrange("p r i -> p (r i)").bitcast(I32))
-        tab_w = tile("tab_w", [P, T], U32)
-        nc.sync.dma_start(tab_w[:].bitcast(I32), tab_words[0].rearrange("p t b -> p (t b)").bitcast(I32))
-        wk_rows = wk_scales.rearrange("a (q r) n -> r q a n", r=4)
-        for r in range(4):
-            nc.sync.dma_start(wk_sc_raw[r:P:32, :, :].bitcast(I32), wk_rows[r].bitcast(I32))
+        nc.vector.memset(tab_sc[0:96, :].bitcast(I32), 0)
+        planes = tile("planes", [P, 2, J + R], U8)
+        nc.vector.memset(planes[:].rearrange("p a j -> p (a j)").bitcast(I32), 0)
 
-        def load_rows(raw, src, a, cols):
+        def load_rows(name, src, a, cols):
+            raw = tile(name, [P, PACK, cols.stop - cols.start], F32)
             nc.sync.dma_start(raw[:], src[a * KP : (a + 1) * KP, cols].rearrange("(p i) c -> p i c", i=PACK))
             return raw
 
@@ -117,33 +122,28 @@ def tile_list_kvt_ts_kernel(
             for c in range(4):
                 col = 4 * g + c
                 nc.tensor.transpose(acc[:, c, :], ts_row[:, col : col + 1].to_broadcast([P, P]), ident[:])
-            copy_on("scalar", ts_by_n[:, :, 4 * g : 4 * g + 4], acc[:].rearrange("p c n -> p n c"))
+            nc.scalar.copy(ts_by_n[:, :, 4 * g : 4 * g + 4], acc[:].rearrange("p c n -> p n c"))
 
-        wk_q = {}
+        both_rows = tile("both_rows", [P, J + R], U8)
+        nc.vector.tensor_copy(
+            both_rows[96:P, J:].bitcast(I32).rearrange("p (b t g) -> p b g t", t=4, g=32),
+            wk_rows[96:P, :].bitcast(I32).rearrange("p (b g t) -> p b g t", t=4, g=32),
+        )
+        sc_rows = tile("sc_rows", [P, J], U8)
+        nc.vector.tensor_copy(sc_rows[:], tab_sc[:].indirect(offsets[:]))
+        nc.vector.tensor_copy(both_rows[96:P, 0:J].bitcast(I32), sc_rows[96:P, :].bitcast(I32))
+        for q in range(4):
+            nc.sync.dma_start(planes[32 * q : 32 * q + 4, :, :].bitcast(I32), both_rows[96 + 8 * q : 96 + 8 * q + 8, :].bitcast(I32))
+        x_raw = [load_rows("x_raw%d" % a, x, a, slice(0, M)) for a in range(2)]
+        half = [slice(0, KP), slice(KP, 2 * KP)]
+        wq_raw = {(a, 0): load_rows("wq_raw%d0" % a, wq, a, half[0]) for a in range(2)}
 
-        def order_wk(a, raw):
-            wk_q[a] = tile("wk_q%d" % a, [P, R], I32)
+        wk_q = tile("wk_q", [P, 2, R], I32)
+
+        def order_wk(a):
             nc.vector.tensor_copy(
-                wk_q[a][:].rearrange("p (b t g i) -> p b t g i", b=2, t=4, i=8),
-                raw[:].rearrange("p (b g t i) -> p b t g i", b=2, t=4, i=8),
-            )
-
-        order_wk(0, wk_raw0)
-        wv_raw0 = load_rows(tile("wv_raw0", [P, PACK, N], F32), wv, 0, slice(0, N))
-        v_sc0 = tile("v_sc0", [P, J], U8)
-        nc.vector.tensor_copy(v_sc0[:], tab_sc[:].indirect(offsets[:]))
-        nc.sync.dma_start(v_sc1[0 : P - 16, :].bitcast(I32), v_sc0[16:P, :].bitcast(I32))
-        v_sc = [v_sc0, v_sc1]
-        wv_raw = [wv_raw0, load_rows(tile("wv_raw1", [P, PACK, N], F32), wv, 1, slice(0, N))]
-        order_wk(1, wk_raw1)
-        x_raw0 = load_rows(tile("x_raw0", [P, PACK, M], F32), x, 0, slice(0, M))
-
-        wk_sc = tile("wk_sc", [P, 2, R], U8)
-
-        def order_wk_scales():
-            nc.vector.tensor_copy(
-                wk_sc[:].rearrange("p a r -> p (a r)").bitcast(I32).rearrange("p (s t g h) -> p s t g h", t=4, g=16, h=2),
-                wk_sc_raw[:].rearrange("p a r -> p (a r)").bitcast(I32).rearrange("p (s g t h) -> p s t g h", t=4, g=16, h=2),
+                wk_q[:, a, :].rearrange("p (b t g u) -> p b t g u", b=2, t=4, u=4),
+                wk_raw[:, a, :].rearrange("p (b g t u) -> p b t g u", b=2, t=4, u=4),
             )
 
         v_pair = {}
@@ -153,10 +153,20 @@ def tile_list_kvt_ts_kernel(
             v_pair[h] = tile("v_pair%d" % h, [P, BANK], U32)
             nc.vector.tensor_copy(v_pair[h][:], tab_w[:].indirect(offsets[:, 32 * h : 32 * (h + 1)]))
 
-        def part_words(h, j0, j1):
-            nc.vector.tensor_copy(
-                v_q[h][:, :, j0:j1], v_pair[h][:, j0:j1].bitcast(U16).rearrange("p (j d) -> p d j", d=2)
-            )
+        def parted(h):
+            return v_pair[h][:].bitcast(U16).rearrange("p (j d) -> p d j", d=2)
+
+        gather_words(0)
+        for a in range(2):
+            nc.vector.tensor_copy(v_q[0][:, a, :], parted(0)[:, a, :])
+            order_wk(a)
+        wq_raw[0, 1] = load_rows("wq_raw01", wq, 0, half[1])
+        gather_words(1)
+        wq_raw[1, 1] = load_rows("wq_raw11", wq, 1, half[1])
+        wv_raw = [load_rows("wv_raw%d" % a, wv, a, slice(0, N)) for a in range(2)]
+        ts_g = tile("ts_g", [P, J], F32)
+        nc.vector.tensor_copy(ts_g[:], ts_win[:].indirect(offsets[:]))
+        nc.vector.tensor_copy(v_q[1][:], parted(1))
 
         def quantize(name, rounded, cols):
             codes = tile(name + "_q", [P, cols], U32)
@@ -164,27 +174,16 @@ def tile_list_kvt_ts_kernel(
             nc.vector.quantize_mx(out=codes[:].bitcast(FP8X4), scales=scales[:], in_=rounded)
             return codes, scales
 
-        def round_plain(name, raw, cols, engine):
-            rounded = tile(name + "_bf", [P, cols * PACK], BF16)
-            copy_on(
-                engine,
-                rounded[:].rearrange("p (c u i) -> p c i u", u=4, i=PACK),
-                raw.rearrange("p i (c u) -> p c i u", u=4),
+        def round_plain(copy, rounded, raw):
+            copy(rounded.rearrange("p (c u i) -> p c i u", u=4, i=PACK), raw.rearrange("p i (c u) -> p c i u", u=4))
+
+        def round_wq(a, b):
+            rounded = tile("wq%d%d_bf" % (a, b), [P, KP * PACK], BF16)
+            nc.vector.tensor_copy(
+                rounded[:].rearrange("p (t g u i) -> p t g i u", t=4, u=4, i=PACK),
+                wq_raw[a, b][:].rearrange("p i (g t u) -> p t g i u", t=4, u=4),
             )
             return rounded
-
-        def round_wq(a, b, engines):
-            rounded = tile("wq%d%d_bf" % (a, b), [P, KP * PACK], BF16)
-            for h in range(2):
-                copy_on(
-                    engines[h],
-                    rounded[:].rearrange("p (t g h u i) -> p h t g i u", g=16, h=2, u=4, i=PACK)[:, h],
-                    wq_raw[a, b][:].rearrange("p i (g t h u) -> p h t g i u", t=4, h=2, u=4)[:, h],
-                )
-            return rounded
-
-        def quantize_wq(a, b, rounded):
-            wq_q[a, b] = quantize("wq%d%d" % (a, b), rounded[:], KP)
 
         kr_bf = {(b, h): tile("kr_bf%d%d" % (b, h), [P, BANK, PACK], BF16) for b in range(2) for h in range(2)}
 
@@ -192,16 +191,16 @@ def tile_list_kvt_ts_kernel(
             acc = bank([P, 4, P])
             cols = slice(c * P, (c + 1) * P)
             jcols = slice(h * BANK + c * P, h * BANK + (c + 1) * P)
-            for t in range(4):
-                for a in range(2):
+            for a in range(2):
+                for t in range(4):
                     nc.tensor.matmul_mx(
                         out=acc[:, t, :],
-                        lhsT=wk_q[a][:, b * KP + t * P : b * KP + (t + 1) * P].bitcast(FP8X4),
-                        lhsT_scale=wk_sc[:, a, b * KP + t * P : b * KP + (t + 1) * P],
+                        lhsT=wk_q[:, a, b * KP + t * P : b * KP + (t + 1) * P].bitcast(FP8X4),
+                        lhsT_scale=planes[:, a, J + b * KP + t * P : J + b * KP + (t + 1) * P],
                         rhs=v_q[h][:, a, cols].bitcast(FP4X4),
-                        rhs_scale=v_sc[a][:, jcols],
-                        start=(a == 0),
-                        stop=(a == 1),
+                        rhs_scale=planes[:, a, jcols],
+                        start=(a == 0 and t == 0),
+                        stop=(a == 1 and t == 3),
                     )
             nc.scalar.copy(kr_bf[b, h][:, cols, :], acc[:].rearrange("p t n -> p n t"))
 
@@ -210,49 +209,28 @@ def tile_list_kvt_ts_kernel(
         def quantize_kr(b, h):
             kr_q[b, h] = quantize("kr%d%d" % (b, h), kr_bf[b, h][:].rearrange("p n t -> p (n t)"), BANK)
 
-        x_q = {}
-        wq_q = {}
-        wq_raw = {}
-        half = [slice(0, KP), slice(KP, 2 * KP)]
-        both_vector = ("vector", "vector")
-        wv_q = {}
-        ts_g = tile("ts_g", [P, J], F32)
-        nc.vector.tensor_copy(ts_g[:], ts_win[:].indirect(offsets[:]))
-        x_raw1 = load_rows(tile("x_raw1", [P, PACK, M], F32), x, 1, slice(0, M))
-        wq_raw[0, 0] = load_rows(tile("wq_raw00", [P, PACK, KP], F32), wq, 0, half[0])
-        wv_bf0 = round_plain("wv0", wv_raw[0][:], N, "scalar")
-        wv_bf1 = round_plain("wv1", wv_raw[1][:], N, "scalar")
-        gather_words(0)
-        order_wk_scales()
-        part_words(0, 0, P)
-        part_words(0, P, BANK)
-        gather_words(1)
-        wq_raw[1, 0] = load_rows(tile("wq_raw10", [P, PACK, KP], F32), wq, 1, half[0])
-        part_words(1, 0, BANK)
-        wq_raw[0, 1] = load_rows(tile("wq_raw01", [P, PACK, KP], F32), wq, 0, half[1])
-        wv_q[0] = quantize("wv0", wv_bf0[:], N)
-        wv_q[1] = quantize("wv1", wv_bf1[:], N)
-        for b in range(2):
-            for h in range(2):
+        x_bf = [tile("x%d_bf" % a, [P, M * PACK], BF16) for a in range(2)]
+        round_plain(nc.scalar.copy, x_bf[0][:], x_raw[0][:])
+        for h in range(2):
+            for b in range(2):
                 for c in range(4):
                     kr_bank(b, h, c)
-        x_bf0 = round_plain("x0", x_raw0[:], M, "vector")
-        wq_raw[1, 1] = load_rows(tile("wq_raw11", [P, PACK, KP], F32), wq, 1, half[1])
-        x_bf1 = round_plain("x1", x_raw1[:], M, "vector")
-        x_q[0] = quantize("x0", x_bf0[:], M)
-        wq_bf00 = round_wq(0, 0, both_vector)
-        x_q[1] = quantize("x1", x_bf1[:], M)
-        quantize_wq(0, 0, wq_bf00)
-        wq_bf10 = round_wq(1, 0, both_vector)
-        quantize_wq(1, 0, wq_bf10)
-        wq_bf01 = round_wq(0, 1, both_vector)
-        quantize_wq(0, 1, wq_bf01)
-        wq_bf11 = round_wq(1, 1, both_vector)
-        quantize_kr(0, 0)
-        quantize_wq(1, 1, wq_bf11)
-        quantize_kr(1, 0)
 
-        qr_bf = tile("qr_bf", [P, 4, 2, P, PACK], BF16)
+        x_q = {}
+        wq_q = {}
+        round_plain(nc.vector.tensor_copy, x_bf[1][:], x_raw[1][:])
+        rounded = round_wq(0, 0)
+        x_q[1] = quantize("x1", x_bf[1][:], M)
+        wq_q[0, 0] = quantize("wq00", rounded[:], KP)
+        rounded = round_wq(1, 0)
+        x_q[0] = quantize("x0", x_bf[0][:], M)
+        wq_q[1, 0] = quantize("wq10", rounded[:], KP)
+        for a in range(2):
+            rounded = round_wq(a, 1)
+            quantize_kr(a, 0)
+            wq_q[a, 1] = quantize("wq%d1" % a, rounded[:], KP)
+
+        qr_bf = [tile("qr_bf%d" % b, [P, M, PACK], BF16) for b in range(2)]
 
         def qr_pass(acc, a, b, m):
             cols = slice(m * P, (m + 1) * P)
@@ -268,70 +246,85 @@ def tile_list_kvt_ts_kernel(
                 )
 
         def qr_out(acc, b, m):
-            nc.scalar.copy(qr_bf[:, m, b, :, :], acc[:].rearrange("p t n -> p n t"))
+            nc.scalar.copy(qr_bf[b][:, m * P : (m + 1) * P, :], acc[:].rearrange("p t n -> p n t"))
 
-        qr_q = {}
-
-        def quantize_qr(m):
-            qr_q[m] = quantize("qr%d" % m, qr_bf[:, m].rearrange("p b n t -> p (b n t)"), 2 * P)
-
-        def scores(m, h):
-            res = tile("sc%d%d" % (m, h), [P, BANK], F32)
-            acc = bank([P, BANK])
-            for b in range(2):
-                nc.tensor.matmul_mx(
-                    out=acc[:],
-                    lhsT=qr_q[m][0][:, b * P : (b + 1) * P].bitcast(FP8X4),
-                    lhsT_scale=qr_q[m][1][:, b * P : (b + 1) * P],
-                    rhs=kr_q[b, h][0][:].bitcast(FP8X4),
-                    rhs_scale=kr_q[b, h][1][:],
-                    start=(b == 0),
-                    stop=(b == 1),
-                )
-            nc.vector.tensor_tensor(res[:], acc[:], ts_g[:, h * BANK : (h + 1) * BANK], MULT)
-            nc.sync.dma_start(out_0[m * P : (m + 1) * P, h * BANK : (h + 1) * BANK], res[:])
-
-        def values(n, h):
-            res = tile("vv%d%d" % (n, h), [P, BANK], F32)
-            acc = bank([P, BANK])
-            cols = slice(h * BANK, (h + 1) * BANK)
-            for a in range(2):
-                nc.tensor.matmul_mx(
-                    out=acc[:],
-                    lhsT=wv_q[a][0][:, n * P : (n + 1) * P].bitcast(FP8X4),
-                    lhsT_scale=wv_q[a][1][:, n * P : (n + 1) * P],
-                    rhs=v_q[h][:, a, :].bitcast(FP4X4),
-                    rhs_scale=v_sc[a][:, cols],
-                    start=(a == 0),
-                    stop=(a == 1),
-                )
-            nc.scalar.copy(res[:], acc[:])
-            nc.sync.dma_start(out_1[n * P : (n + 1) * P, cols], res[:])
-
-        for n in range(2):
-            for h in range(2):
-                values(n, h)
         for m in range(4):
             acc = bank([P, 4, P])
             qr_pass(acc, 0, 0, m)
             qr_pass(acc, 1, 0, m)
             qr_out(acc, 0, m)
+        wv_bf = tile("wv_bf", [P, 2, N * PACK], BF16)
+        for a in range(2):
+            round_plain(nc.scalar.copy, wv_bf[:, a, :], wv_raw[a][:])
         accs = [bank([P, 4, P]) for m in range(4)]
         for m in range(4):
             qr_pass(accs[m], 0, 1, m)
         for m in range(4):
             qr_pass(accs[m], 1, 1, m)
             qr_out(accs[m], 1, m)
-        quantize_kr(0, 1)
-        quantize_qr(0)
-        quantize_qr(1)
-        scores(0, 0)
-        quantize_kr(1, 1)
-        scores(1, 0)
-        quantize_qr(2)
-        scores(0, 1)
-        quantize_qr(3)
-        scores(1, 1)
-        for m in range(2, 4):
-            for h in range(2):
-                scores(m, h)
+
+        wv_q = quantize("wv", wv_bf[:].rearrange("p a c -> p (a c)"), 2 * N)
+        qr0 = quantize("qr0", qr_bf[0][:].rearrange("p n t -> p (n t)"), M)
+        qr_q = {(0, m): (qr0[0][:, m * P : (m + 1) * P], qr0[1][:, m * P : (m + 1) * P]) for m in range(4)}
+
+        def quantize_qr1(m):
+            codes, scales = quantize("qr1%d" % m, qr_bf[1][:, m * P : (m + 1) * P, :].rearrange("p n t -> p (n t)"), P)
+            qr_q[1, m] = (codes[:], scales[:])
+
+        results = []
+
+        def result():
+            results.append(tile("res%d" % len(results), [P, BANK], F32))
+            return results[-1]
+
+        def score_pass(acc, b, m, h):
+            nc.tensor.matmul_mx(
+                out=acc[:],
+                lhsT=qr_q[b, m][0].bitcast(FP8X4),
+                lhsT_scale=qr_q[b, m][1],
+                rhs=kr_q[b, h][0][:].bitcast(FP8X4),
+                rhs_scale=kr_q[b, h][1][:],
+                start=(b == 0),
+                stop=(b == 1),
+            )
+
+        def score_out(acc, m, h):
+            res = result()
+            nc.vector.tensor_tensor(res[:], acc[:], ts_g[:, h * BANK : (h + 1) * BANK], MULT)
+            nc.sync.dma_start(out_0[m * P : (m + 1) * P, h * BANK : (h + 1) * BANK], res[:])
+
+        def scores(m, h):
+            acc = bank([P, BANK])
+            for b in range(2):
+                score_pass(acc, b, m, h)
+            score_out(acc, m, h)
+
+        def values(n, h):
+            res = result()
+            acc = bank([P, BANK])
+            cols = slice(h * BANK, (h + 1) * BANK)
+            for a in range(2):
+                ncols = slice(a * N + n * P, a * N + (n + 1) * P)
+                nc.tensor.matmul_mx(
+                    out=acc[:],
+                    lhsT=wv_q[0][:, ncols].bitcast(FP8X4),
+                    lhsT_scale=wv_q[1][:, ncols],
+                    rhs=v_q[h][:, a, :].bitcast(FP4X4),
+                    rhs_scale=planes[:, a, cols],
+                    start=(a == 0),
+                    stop=(a == 1),
+                )
+            nc.scalar.copy(res[:], acc[:])
+            nc.sync.dma_start(out_1[n * P : (n + 1) * P, cols], res[:])
+
+        for h in range(2):
+            values(0, h)
+        for m in range(4):
+            quantize_qr1(m)
+            if m < 2:
+                quantize_kr(m, 1)
+            scores(m, 0)
+        for m in range(4):
+            scores(m, 1)
+        for h in range(2):
+            values(1, h)

@@ -32,15 +32,11 @@ def tile_list_kvt_ts_kernel(
         psum = ctx.enter_context(tc.psum_pool(name="psum", bufs=1))
 
         chains = [
-            [("ts_g", 4096), ("wk_raw", 8192), ("room", 4096)],
-            [("x_raw0", 8192), ("sc_rows", J), ("x_raw1", 8192)],
+            [("wk_q0", 4096), ("tab_sc", T), ("x0_bf", 4096), ("sc_rows", J)],
+            [("x_raw1", 8192), ("x_raw0", 8192), ("ts_g", 4 * J), ("wk_raw0", 4096), ("wv_raw0", 4096 + 2 * LAP)],
             [("wq_raw00", 8192), ("both_rows", J + R), ("wq_raw10", 8192)],
-            [("wq_raw01", 8192), ("v_pair0", 2048)],
-            [("wq_raw11", 8192), ("tab_w", 4 * T), ("wv_raw1", 4096)],
-            [("wq10_q", 2048), ("wv_bf", 4096)],
-            [("kr_bf00", 4096)],
-            [("kr_bf10", 4096)],
-            [("kr_bf01", 4096)],
+            [("ts_win", 4 * T)],
+            [("wq_raw11", 8192), ("tab_w", 4 * T), ("wq_raw01", 8192)],
         ]
         where = {}
         end = 0
@@ -49,25 +45,25 @@ def tile_list_kvt_ts_kernel(
                 where[name] = end
                 end = end + size - LAP
             end = end + LAP
-        where["v_pair1"] = where["wk_raw"] + 4096
-        where["x1_bf"] = where["v_pair1"] + 2048 - LAP
-        where["wv_raw0"] = where["tab_w"] + LAP
-        where["x0_bf"] = where["wv_raw0"] + 4096
-        where["wq00_bf"] = where["wk_raw"] + LAP
-        where["qr0_q"] = where["kr_bf10"] + 2048
-        where["kr11_q"] = where["wq_raw11"] + 4096
-        for later, earlier in [
-            ("wk_rows", "sc_rows"),
-            ("wq10_bf", "x1_bf"),
-            ("x0_q", "wq00_bf"),
-            ("wq01_bf", "x0_bf"),
-            ("kr00_q", "wq10_bf"),
-            ("wq11_bf", "kr_bf00"),
-            ("kr10_q", "wq01_bf"),
-            ("wv_q", "kr_bf10"),
-            ("kr01_q", "wq_raw11"),
+        where["wv_raw1"] = where["x0_bf"]
+        where["wk_q1"] = where["ts_win"]
+        where["v_pair0"] = where["wk_q1"] + 4096 - LAP
+        for host, guests in [
+            ("x_raw0", [("wk_raw1", 4096)]),
+            ("wv_raw0", [("kr_bf10", 0)]),
+            ("tab_w", [("x1_bf", 4096), ("wv_bf", 4096)]),
+            ("x1_bf", [("kr00_q", 2048)]),
+            ("x_raw1", [("wq00_bf", 4096)]),
+            ("wq_raw00", [("kr10_q", 2048), ("wq10_bf", 4096)]),
+            ("wq_raw10", [("wq01_bf", 4096)]),
+            ("wq_raw01", [("kr01_q", 2048), ("wq11_bf", 4096)]),
+            ("wq_raw11", [("kr11_q", 2048), ("qr0_q", 2048)]),
         ]:
-            where[later] = where[earlier]
+            end = where[host] + LAP
+            for name, size in guests:
+                where[name] = end
+                end = end + size
+        where["v_pair1"] = where["wk_raw1"] + 4096 - LAP
 
         def tile(name, shape, dtype):
             if name in where:
@@ -88,11 +84,21 @@ def tile_list_kvt_ts_kernel(
         nc.sync.dma_start(tab_sc[96:P, :].bitcast(I32), tab_scales.rearrange("a q t -> q a t").bitcast(I32))
         wk_rows = tile("wk_rows", [P, R], U8)
         nc.sync.dma_start(wk_rows[96:P, :].bitcast(I32), wk_scales.rearrange("a q r -> q a r").bitcast(I32))
+
+        def load_rows(name, src, a, cols):
+            raw = tile(name, [P, PACK, cols.stop - cols.start], F32)
+            nc.sync.dma_start(raw[:], src[a * KP : (a + 1) * KP, cols].rearrange("(p i) c -> p i c", i=PACK))
+            return raw
+
+        def load_wk(b):
+            raw = tile("wk_raw%d" % b, [P, 2, KP], I32)
+            nc.sync.dma_start(raw[:], wk_words[:, :, b * KP : (b + 1) * KP, :].rearrange("a p r i -> p a (r i)").bitcast(I32))
+            return raw
+
+        x_raw = [load_rows("x_raw0", x, 0, slice(0, M))]
+        wk_raw = [load_wk(0)]
         tab_w = tile("tab_w", [P, T], U32)
         nc.sync.dma_start(tab_w[:].bitcast(I32), tab_words[0].rearrange("p t b -> p (t b)").bitcast(I32))
-        wk_raw = tile("wk_raw", [P, 2, R], I32)
-        for a in range(2):
-            nc.sync.dma_start(wk_raw[:, a, :], wk_words[a].rearrange("p r i -> p (r i)").bitcast(I32))
 
         ones = tile("ones", [P, P], F32)
         ident = tile("ident", [P, P], F32)
@@ -110,11 +116,6 @@ def tile_list_kvt_ts_kernel(
         planes = tile("planes", [P, 2, J + R], U8)
         nc.vector.memset(planes[:].rearrange("p a j -> p (a j)").bitcast(I32), 0)
 
-        def load_rows(name, src, a, cols):
-            raw = tile(name, [P, PACK, cols.stop - cols.start], F32)
-            nc.sync.dma_start(raw[:], src[a * KP : (a + 1) * KP, cols].rearrange("(p i) c -> p i c", i=PACK))
-            return raw
-
         ts_win = tile("ts_win", [P, T], F32)
         ts_by_n = ts_win[:].rearrange("p (n c) -> p n c", n=P)
         for g in range(T // P // 4):
@@ -124,27 +125,52 @@ def tile_list_kvt_ts_kernel(
                 nc.tensor.transpose(acc[:, c, :], ts_row[:, col : col + 1].to_broadcast([P, P]), ident[:])
             nc.scalar.copy(ts_by_n[:, :, 4 * g : 4 * g + 4], acc[:].rearrange("p c n -> p n c"))
 
+        sc_rows = tile("sc_rows", [P, J], U8)
+        nc.vector.tensor_copy(sc_rows[:], tab_sc[:].indirect(offsets[:]))
         both_rows = tile("both_rows", [P, J + R], U8)
         nc.vector.tensor_copy(
             both_rows[96:P, J:].bitcast(I32).rearrange("p (b t g) -> p b g t", t=4, g=32),
             wk_rows[96:P, :].bitcast(I32).rearrange("p (b g t) -> p b g t", t=4, g=32),
         )
-        sc_rows = tile("sc_rows", [P, J], U8)
-        nc.vector.tensor_copy(sc_rows[:], tab_sc[:].indirect(offsets[:]))
         nc.vector.tensor_copy(both_rows[96:P, 0:J].bitcast(I32), sc_rows[96:P, :].bitcast(I32))
         for q in range(4):
             nc.sync.dma_start(planes[32 * q : 32 * q + 4, :, :].bitcast(I32), both_rows[96 + 8 * q : 96 + 8 * q + 8, :].bitcast(I32))
-        x_raw = [load_rows("x_raw%d" % a, x, a, slice(0, M)) for a in range(2)]
+
+        def quantize(name, rounded, cols):
+            codes = tile(name + "_q", [P, cols], U32)
+            scales = tile(name + "_s", [P, cols], U8)
+            nc.vector.quantize_mx(out=codes[:].bitcast(FP8X4), scales=scales[:], in_=rounded)
+            return codes, scales
+
+        def round_plain(copy, rounded, raw):
+            copy(rounded.rearrange("p (c u i) -> p c i u", u=4, i=PACK), raw.rearrange("p i (c u) -> p c i u", u=4))
+
+        def round_x(a):
+            rounded = tile("x%d_bf" % a, [P, M * PACK], BF16)
+            round_plain(nc.vector.tensor_copy, rounded[:], x_raw[a][:])
+            return rounded
+
+        wk_q = {}
+
+        def order_wk(b):
+            wk_q[b] = tile("wk_q%d" % b, [P, 2, KP], I32)
+            nc.vector.tensor_copy(
+                wk_q[b][:].rearrange("p a (t g u) -> p a t g u", t=4, u=4),
+                wk_raw[b][:].rearrange("p a (g t u) -> p a t g u", t=4, u=4),
+            )
+
+        x_q = {}
+        wq_q = {}
+        rounded = round_x(0)
+        wk_raw.append(load_wk(1))
+        x_raw.append(load_rows("x_raw1", x, 1, slice(0, M)))
+        order_wk(0)
+        x_q[0] = quantize("x0", rounded[:], M)
+        wv_raw = [load_rows("wv_raw%d" % a, wv, a, slice(0, N)) for a in range(2)]
         half = [slice(0, KP), slice(KP, 2 * KP)]
         wq_raw = {(a, 0): load_rows("wq_raw%d0" % a, wq, a, half[0]) for a in range(2)}
-
-        wk_q = tile("wk_q", [P, 2, R], I32)
-
-        def order_wk(a):
-            nc.vector.tensor_copy(
-                wk_q[:, a, :].rearrange("p (b t g u) -> p b t g u", b=2, t=4, u=4),
-                wk_raw[:, a, :].rearrange("p (b g t u) -> p b t g u", b=2, t=4, u=4),
-            )
+        ts_g = tile("ts_g", [P, J], F32)
+        nc.vector.tensor_copy(ts_g[:], ts_win[:].indirect(offsets[:]))
 
         v_pair = {}
         v_q = [tile("v_q%d" % h, [P, 2, BANK], U16) for h in range(2)]
@@ -157,25 +183,12 @@ def tile_list_kvt_ts_kernel(
             return v_pair[h][:].bitcast(U16).rearrange("p (j d) -> p d j", d=2)
 
         gather_words(0)
-        for a in range(2):
-            nc.vector.tensor_copy(v_q[0][:, a, :], parted(0)[:, a, :])
-            order_wk(a)
-        wq_raw[0, 1] = load_rows("wq_raw01", wq, 0, half[1])
+        nc.vector.tensor_copy(v_q[0][:, :, 0:P], parted(0)[:, :, 0:P])
+        nc.vector.tensor_copy(v_q[0][:, :, P:BANK], parted(0)[:, :, P:BANK])
+        order_wk(1)
         gather_words(1)
-        wq_raw[1, 1] = load_rows("wq_raw11", wq, 1, half[1])
-        wv_raw = [load_rows("wv_raw%d" % a, wv, a, slice(0, N)) for a in range(2)]
-        ts_g = tile("ts_g", [P, J], F32)
-        nc.vector.tensor_copy(ts_g[:], ts_win[:].indirect(offsets[:]))
-        nc.vector.tensor_copy(v_q[1][:], parted(1))
-
-        def quantize(name, rounded, cols):
-            codes = tile(name + "_q", [P, cols], U32)
-            scales = tile(name + "_s", [P, cols], U8)
-            nc.vector.quantize_mx(out=codes[:].bitcast(FP8X4), scales=scales[:], in_=rounded)
-            return codes, scales
-
-        def round_plain(copy, rounded, raw):
-            copy(rounded.rearrange("p (c u i) -> p c i u", u=4, i=PACK), raw.rearrange("p i (c u) -> p c i u", u=4))
+        for a in range(2):
+            wq_raw[a, 1] = load_rows("wq_raw%d1" % a, wq, a, half[1])
 
         def round_wq(a, b):
             rounded = tile("wq%d%d_bf" % (a, b), [P, KP * PACK], BF16)
@@ -195,7 +208,7 @@ def tile_list_kvt_ts_kernel(
                 for t in range(4):
                     nc.tensor.matmul_mx(
                         out=acc[:, t, :],
-                        lhsT=wk_q[:, a, b * KP + t * P : b * KP + (t + 1) * P].bitcast(FP8X4),
+                        lhsT=wk_q[b][:, a, t * P : (t + 1) * P].bitcast(FP8X4),
                         lhsT_scale=planes[:, a, J + b * KP + t * P : J + b * KP + (t + 1) * P],
                         rhs=v_q[h][:, a, cols].bitcast(FP4X4),
                         rhs_scale=planes[:, a, jcols],
@@ -209,26 +222,58 @@ def tile_list_kvt_ts_kernel(
         def quantize_kr(b, h):
             kr_q[b, h] = quantize("kr%d%d" % (b, h), kr_bf[b, h][:].rearrange("p n t -> p (n t)"), BANK)
 
-        x_bf = [tile("x%d_bf" % a, [P, M * PACK], BF16) for a in range(2)]
-        round_plain(nc.scalar.copy, x_bf[0][:], x_raw[0][:])
+        x1_bf = round_x(1)
+        nc.vector.tensor_copy(v_q[1][:], parted(1))
+        wv_bf = tile("wv_bf", [P, 2, N * PACK], BF16)
         for h in range(2):
             for b in range(2):
                 for c in range(4):
                     kr_bank(b, h, c)
+                if (h, b) == (0, 0):
+                    round_plain(nc.scalar.copy, wv_bf[:, 0, :], wv_raw[0][:])
 
-        x_q = {}
-        wq_q = {}
-        round_plain(nc.vector.tensor_copy, x_bf[1][:], x_raw[1][:])
+        x_q[1] = quantize("x1", x1_bf[:], M)
+        round_plain(nc.vector.tensor_copy, wv_bf[:, 1, :], wv_raw[1][:])
+        quantize_kr(0, 0)
         rounded = round_wq(0, 0)
-        x_q[1] = quantize("x1", x_bf[1][:], M)
+        wv_q = quantize("wv", wv_bf[:].rearrange("p a c -> p (a c)"), 2 * N)
         wq_q[0, 0] = quantize("wq00", rounded[:], KP)
         rounded = round_wq(1, 0)
-        x_q[0] = quantize("x0", x_bf[0][:], M)
+        quantize_kr(1, 0)
         wq_q[1, 0] = quantize("wq10", rounded[:], KP)
-        for a in range(2):
-            rounded = round_wq(a, 1)
-            quantize_kr(a, 0)
-            wq_q[a, 1] = quantize("wq%d1" % a, rounded[:], KP)
+        rounded = round_wq(0, 1)
+        quantize_kr(0, 1)
+        wq_q[0, 1] = quantize("wq01", rounded[:], KP)
+        rounded = round_wq(1, 1)
+        wq_q[1, 1] = quantize("wq11", rounded[:], KP)
+
+        results = []
+
+        def result():
+            results.append(tile("res%d" % len(results), [P, BANK], F32))
+            return results[-1]
+
+        def values(n, h):
+            res = result()
+            acc = bank([P, BANK])
+            cols = slice(h * BANK, (h + 1) * BANK)
+            for a in range(2):
+                ncols = slice(a * N + n * P, a * N + (n + 1) * P)
+                nc.tensor.matmul_mx(
+                    out=acc[:],
+                    lhsT=wv_q[0][:, ncols].bitcast(FP8X4),
+                    lhsT_scale=wv_q[1][:, ncols],
+                    rhs=v_q[h][:, a, :].bitcast(FP4X4),
+                    rhs_scale=planes[:, a, cols],
+                    start=(a == 0),
+                    stop=(a == 1),
+                )
+            nc.scalar.copy(res[:], acc[:])
+            nc.sync.dma_start(out_1[n * P : (n + 1) * P, cols], res[:])
+
+        for n in range(2):
+            for h in range(2):
+                values(n, h)
 
         qr_bf = [tile("qr_bf%d" % b, [P, M, PACK], BF16) for b in range(2)]
 
@@ -253,9 +298,6 @@ def tile_list_kvt_ts_kernel(
             qr_pass(acc, 0, 0, m)
             qr_pass(acc, 1, 0, m)
             qr_out(acc, 0, m)
-        wv_bf = tile("wv_bf", [P, 2, N * PACK], BF16)
-        for a in range(2):
-            round_plain(nc.scalar.copy, wv_bf[:, a, :], wv_raw[a][:])
         accs = [bank([P, 4, P]) for m in range(4)]
         for m in range(4):
             qr_pass(accs[m], 0, 1, m)
@@ -263,19 +305,13 @@ def tile_list_kvt_ts_kernel(
             qr_pass(accs[m], 1, 1, m)
             qr_out(accs[m], 1, m)
 
-        wv_q = quantize("wv", wv_bf[:].rearrange("p a c -> p (a c)"), 2 * N)
+        quantize_kr(1, 1)
         qr0 = quantize("qr0", qr_bf[0][:].rearrange("p n t -> p (n t)"), M)
         qr_q = {(0, m): (qr0[0][:, m * P : (m + 1) * P], qr0[1][:, m * P : (m + 1) * P]) for m in range(4)}
 
         def quantize_qr1(m):
             codes, scales = quantize("qr1%d" % m, qr_bf[1][:, m * P : (m + 1) * P, :].rearrange("p n t -> p (n t)"), P)
             qr_q[1, m] = (codes[:], scales[:])
-
-        results = []
-
-        def result():
-            results.append(tile("res%d" % len(results), [P, BANK], F32))
-            return results[-1]
 
         def score_pass(acc, b, m, h):
             nc.tensor.matmul_mx(
@@ -299,32 +335,8 @@ def tile_list_kvt_ts_kernel(
                 score_pass(acc, b, m, h)
             score_out(acc, m, h)
 
-        def values(n, h):
-            res = result()
-            acc = bank([P, BANK])
-            cols = slice(h * BANK, (h + 1) * BANK)
-            for a in range(2):
-                ncols = slice(a * N + n * P, a * N + (n + 1) * P)
-                nc.tensor.matmul_mx(
-                    out=acc[:],
-                    lhsT=wv_q[0][:, ncols].bitcast(FP8X4),
-                    lhsT_scale=wv_q[1][:, ncols],
-                    rhs=v_q[h][:, a, :].bitcast(FP4X4),
-                    rhs_scale=planes[:, a, cols],
-                    start=(a == 0),
-                    stop=(a == 1),
-                )
-            nc.scalar.copy(res[:], acc[:])
-            nc.sync.dma_start(out_1[n * P : (n + 1) * P, cols], res[:])
-
-        for h in range(2):
-            values(0, h)
         for m in range(4):
             quantize_qr1(m)
-            if m < 2:
-                quantize_kr(m, 1)
             scores(m, 0)
         for m in range(4):
             scores(m, 1)
-        for h in range(2):
-            values(1, h)

@@ -32,10 +32,10 @@ def tile_list_kvt_ts_kernel(
         psum = ctx.enter_context(tc.psum_pool(name="psum", bufs=1))
 
         chains = [
-            [("wk_q0", 4096), ("tab_sc", T), ("x0_bf", 4096), ("sc_rows", J)],
-            [("x_raw1", 8192), ("x_raw0", 8192), ("ts_g", 4 * J), ("wk_raw0", 4096), ("wv_raw0", 4096 + 2 * LAP)],
-            [("wq_raw00", 8192), ("both_rows", J + R), ("wq_raw10", 8192)],
-            [("ts_win", 4 * T)],
+            [("wk_raw1", 4096), ("wk_raw0", 4096), ("wk_rows", R), ("wv_raw0", 4096)],
+            [("wv_raw1", 4096), ("sc_rows", J), ("x_raw0", 8192)],
+            [("x_raw1", 8192), ("both_rows", J + R)],
+            [("wq_raw00", 8192), ("v_pair0", 2048), ("wq_raw10", 8192)],
             [("wq_raw11", 8192), ("tab_w", 4 * T), ("wq_raw01", 8192)],
         ]
         where = {}
@@ -45,25 +45,21 @@ def tile_list_kvt_ts_kernel(
                 where[name] = end
                 end = end + size - LAP
             end = end + LAP
-        where["wv_raw1"] = where["x0_bf"]
-        where["wk_q1"] = where["ts_win"]
-        where["v_pair0"] = where["wk_q1"] + 4096 - LAP
+        where["kr_bf00"] = where["wv_raw1"]
         for host, guests in [
-            ("x_raw0", [("wk_raw1", 4096)]),
-            ("wv_raw0", [("kr_bf10", 0)]),
-            ("tab_w", [("x1_bf", 4096), ("wv_bf", 4096)]),
-            ("x1_bf", [("kr00_q", 2048)]),
-            ("x_raw1", [("wq00_bf", 4096)]),
-            ("wq_raw00", [("kr10_q", 2048), ("wq10_bf", 4096)]),
+            ("wk_raw0", [("v_q0", 2048), ("v_pair1", 2048)]),
+            ("tab_w", [("wk_q1", 4096), ("kr00_q", 2048 - LAP), ("x0_bf", 4096 - LAP), ("x1_bf", 4096)]),
+            ("x_raw0", [("wv_q", 2048)]),
+            ("x_raw1", [("kr01_q", 2048), ("wq00_bf", 4096)]),
+            ("wq_raw00", [("wq10_bf", 4096)]),
             ("wq_raw10", [("wq01_bf", 4096)]),
-            ("wq_raw01", [("kr01_q", 2048), ("wq11_bf", 4096)]),
-            ("wq_raw11", [("kr11_q", 2048), ("qr0_q", 2048)]),
+            ("wq_raw01", [("wq11_bf", 4096)]),
+            ("wq_raw11", [("qr0_q", 2048), ("kr10_q", 2048), ("kr11_q", 2048)]),
         ]:
             end = where[host] + LAP
             for name, size in guests:
                 where[name] = end
                 end = end + size
-        where["v_pair1"] = where["wk_raw1"] + 4096 - LAP
 
         def tile(name, shape, dtype):
             if name in where:
@@ -95,8 +91,6 @@ def tile_list_kvt_ts_kernel(
             nc.sync.dma_start(raw[:], wk_words[:, :, b * KP : (b + 1) * KP, :].rearrange("a p r i -> p a (r i)").bitcast(I32))
             return raw
 
-        x_raw = [load_rows("x_raw0", x, 0, slice(0, M))]
-        wk_raw = [load_wk(0)]
         tab_w = tile("tab_w", [P, T], U32)
         nc.sync.dma_start(tab_w[:].bitcast(I32), tab_words[0].rearrange("p t b -> p (t b)").bitcast(I32))
 
@@ -125,16 +119,20 @@ def tile_list_kvt_ts_kernel(
                 nc.tensor.transpose(acc[:, c, :], ts_row[:, col : col + 1].to_broadcast([P, P]), ident[:])
             nc.scalar.copy(ts_by_n[:, :, 4 * g : 4 * g + 4], acc[:].rearrange("p c n -> p n c"))
 
-        sc_rows = tile("sc_rows", [P, J], U8)
-        nc.vector.tensor_copy(sc_rows[:], tab_sc[:].indirect(offsets[:]))
         both_rows = tile("both_rows", [P, J + R], U8)
         nc.vector.tensor_copy(
             both_rows[96:P, J:].bitcast(I32).rearrange("p (b t g) -> p b g t", t=4, g=32),
             wk_rows[96:P, :].bitcast(I32).rearrange("p (b g t) -> p b g t", t=4, g=32),
         )
+        wk_raw = [load_wk(0)]
+        wv_raw = [load_rows("wv_raw0", wv, 0, slice(0, N))]
+        sc_rows = tile("sc_rows", [P, J], U8)
+        nc.vector.tensor_copy(sc_rows[:], tab_sc[:].indirect(offsets[:]))
         nc.vector.tensor_copy(both_rows[96:P, 0:J].bitcast(I32), sc_rows[96:P, :].bitcast(I32))
         for q in range(4):
             nc.sync.dma_start(planes[32 * q : 32 * q + 4, :, :].bitcast(I32), both_rows[96 + 8 * q : 96 + 8 * q + 8, :].bitcast(I32))
+        wv_raw.append(load_rows("wv_raw1", wv, 1, slice(0, N)))
+        x_raw = [load_rows("x_raw0", x, 0, slice(0, M))]
 
         def quantize(name, rounded, cols):
             codes = tile(name + "_q", [P, cols], U32)
@@ -161,19 +159,9 @@ def tile_list_kvt_ts_kernel(
 
         x_q = {}
         wq_q = {}
-        rounded = round_x(0)
-        wk_raw.append(load_wk(1))
-        x_raw.append(load_rows("x_raw1", x, 1, slice(0, M)))
-        order_wk(0)
-        x_q[0] = quantize("x0", rounded[:], M)
-        wv_raw = [load_rows("wv_raw%d" % a, wv, a, slice(0, N)) for a in range(2)]
         half = [slice(0, KP), slice(KP, 2 * KP)]
-        wq_raw = {(a, 0): load_rows("wq_raw%d0" % a, wq, a, half[0]) for a in range(2)}
-        ts_g = tile("ts_g", [P, J], F32)
-        nc.vector.tensor_copy(ts_g[:], ts_win[:].indirect(offsets[:]))
 
         v_pair = {}
-        v_q = [tile("v_q%d" % h, [P, 2, BANK], U16) for h in range(2)]
 
         def gather_words(h):
             v_pair[h] = tile("v_pair%d" % h, [P, BANK], U32)
@@ -183,12 +171,20 @@ def tile_list_kvt_ts_kernel(
             return v_pair[h][:].bitcast(U16).rearrange("p (j d) -> p d j", d=2)
 
         gather_words(0)
+        order_wk(0)
+        wk_raw.append(load_wk(1))
+        x_raw.append(load_rows("x_raw1", x, 1, slice(0, M)))
+        v_q = [tile("v_q%d" % h, [P, 2, BANK], U16) for h in range(2)]
         nc.vector.tensor_copy(v_q[0][:, :, 0:P], parted(0)[:, :, 0:P])
         nc.vector.tensor_copy(v_q[0][:, :, P:BANK], parted(0)[:, :, P:BANK])
-        order_wk(1)
+        wq_raw = {(a, 0): load_rows("wq_raw%d0" % a, wq, a, half[0]) for a in range(2)}
         gather_words(1)
         for a in range(2):
             wq_raw[a, 1] = load_rows("wq_raw%d1" % a, wq, a, half[1])
+        nc.vector.tensor_copy(v_q[1][:], parted(1))
+        ts_g = tile("ts_g", [P, J], F32)
+        nc.vector.tensor_copy(ts_g[:], ts_win[:].indirect(offsets[:]))
+        order_wk(1)
 
         def round_wq(a, b):
             rounded = tile("wq%d%d_bf" % (a, b), [P, KP * PACK], BF16)
@@ -222,30 +218,26 @@ def tile_list_kvt_ts_kernel(
         def quantize_kr(b, h):
             kr_q[b, h] = quantize("kr%d%d" % (b, h), kr_bf[b, h][:].rearrange("p n t -> p (n t)"), BANK)
 
-        x1_bf = round_x(1)
-        nc.vector.tensor_copy(v_q[1][:], parted(1))
         wv_bf = tile("wv_bf", [P, 2, N * PACK], BF16)
-        for h in range(2):
-            for b in range(2):
+        for a in range(2):
+            round_plain(nc.scalar.copy, wv_bf[:, a, :], wv_raw[a][:])
+        rounded = round_x(0)
+        wv_q = quantize("wv", wv_bf[:].rearrange("p a c -> p (a c)"), 2 * N)
+        x_q[0] = quantize("x0", rounded[:], M)
+        x1_bf = round_x(1)
+        for b in range(2):
+            for h in range(2):
                 for c in range(4):
                     kr_bank(b, h, c)
-                if (h, b) == (0, 0):
-                    round_plain(nc.scalar.copy, wv_bf[:, 0, :], wv_raw[0][:])
 
-        x_q[1] = quantize("x1", x1_bf[:], M)
-        round_plain(nc.vector.tensor_copy, wv_bf[:, 1, :], wv_raw[1][:])
         quantize_kr(0, 0)
+        x_q[1] = quantize("x1", x1_bf[:], M)
         rounded = round_wq(0, 0)
-        wv_q = quantize("wv", wv_bf[:].rearrange("p a c -> p (a c)"), 2 * N)
-        wq_q[0, 0] = quantize("wq00", rounded[:], KP)
-        rounded = round_wq(1, 0)
-        quantize_kr(1, 0)
-        wq_q[1, 0] = quantize("wq10", rounded[:], KP)
-        rounded = round_wq(0, 1)
         quantize_kr(0, 1)
-        wq_q[0, 1] = quantize("wq01", rounded[:], KP)
-        rounded = round_wq(1, 1)
-        wq_q[1, 1] = quantize("wq11", rounded[:], KP)
+        wq_q[0, 0] = quantize("wq00", rounded[:], KP)
+        wq_q[1, 0] = quantize("wq10", round_wq(1, 0)[:], KP)
+        wq_q[0, 1] = quantize("wq01", round_wq(0, 1)[:], KP)
+        wq11_bf = round_wq(1, 1)
 
         results = []
 
@@ -301,12 +293,12 @@ def tile_list_kvt_ts_kernel(
         accs = [bank([P, 4, P]) for m in range(4)]
         for m in range(4):
             qr_pass(accs[m], 0, 1, m)
+        wq_q[1, 1] = quantize("wq11", wq11_bf[:], KP)
         for m in range(4):
             qr_pass(accs[m], 1, 1, m)
             qr_out(accs[m], 1, m)
-
-        quantize_kr(1, 1)
         qr0 = quantize("qr0", qr_bf[0][:].rearrange("p n t -> p (n t)"), M)
+        quantize_kr(1, 0)
         qr_q = {(0, m): (qr0[0][:, m * P : (m + 1) * P], qr0[1][:, m * P : (m + 1) * P]) for m in range(4)}
 
         def quantize_qr1(m):
@@ -324,10 +316,19 @@ def tile_list_kvt_ts_kernel(
                 stop=(b == 1),
             )
 
+        aside = []
+
         def score_out(acc, m, h):
             res = result()
-            nc.vector.tensor_tensor(res[:], acc[:], ts_g[:, h * BANK : (h + 1) * BANK], MULT)
-            nc.sync.dma_start(out_0[m * P : (m + 1) * P, h * BANK : (h + 1) * BANK], res[:])
+            dst = out_0[m * P : (m + 1) * P, h * BANK : (h + 1) * BANK]
+            if (m, h) in aside:
+                plain = result()
+                nc.scalar.copy(plain[:], acc[:])
+                nc.gpsimd.tensor_tensor(res[:], plain[:], ts_g[:, h * BANK : (h + 1) * BANK], MULT)
+                nc.scalar.dma_start(dst, res[:])
+            else:
+                nc.vector.tensor_tensor(res[:], acc[:], ts_g[:, h * BANK : (h + 1) * BANK], MULT)
+                nc.sync.dma_start(dst, res[:])
 
         def scores(m, h):
             acc = bank([P, BANK])
@@ -335,8 +336,13 @@ def tile_list_kvt_ts_kernel(
                 score_pass(acc, b, m, h)
             score_out(acc, m, h)
 
+        early = [bank([P, BANK]) for m in range(4)]
+        for m in range(4):
+            score_pass(early[m], 0, m, 0)
         for m in range(4):
             quantize_qr1(m)
-            scores(m, 0)
-        for m in range(4):
+            if m == 0:
+                quantize_kr(1, 1)
+            score_pass(early[m], 1, m, 0)
+            score_out(early[m], m, 0)
             scores(m, 1)

@@ -33,10 +33,12 @@ def tile_list_kvt_ts_kernel(
 
         chains = [
             [("wk_raw1", 4096), ("wk_raw0", 4096), ("wk_rows", R), ("wv_raw0", 4096)],
-            [("wv_raw1", 4096), ("sc_rows", J), ("x_raw0", 8192)],
+            [("wv_raw1", 4096), ("tab_sc", T)],
+            [("sc_rows", J), ("x_raw0", 8192)],
             [("x_raw1", 8192), ("both_rows", J + R)],
             [("wq_raw00", 8192), ("v_pair0", 2048), ("wq_raw10", 8192)],
-            [("wq_raw11", 8192), ("tab_w", 4 * T), ("wq_raw01", 8192)],
+            [("wq_last0", 4096), ("tab_w", 4 * T), ("wq_raw01", 8192)],
+            [("ts_win", 4 * T)],
         ]
         where = {}
         end = 0
@@ -53,13 +55,14 @@ def tile_list_kvt_ts_kernel(
             ("x_raw1", [("kr01_q", 2048), ("wq00_bf", 4096)]),
             ("wq_raw00", [("wq10_bf", 4096)]),
             ("wq_raw10", [("wq01_bf", 4096)]),
-            ("wq_raw01", [("wq11_bf", 4096)]),
-            ("wq_raw11", [("qr0_q", 2048), ("kr10_q", 2048), ("kr11_q", 2048)]),
+            ("ts_win", [("qr0_q", 2048 - LAP), ("wq_last1", 4096 - LAP), ("kr11_q", 2048)]),
+            ("wq_last1", [("kr10_q", 2048)]),
         ]:
             end = where[host] + LAP
             for name, size in guests:
                 where[name] = end
                 end = end + size
+        where["wq11_bf"] = where["wq10_bf"]
 
         def tile(name, shape, dtype):
             if name in where:
@@ -128,10 +131,10 @@ def tile_list_kvt_ts_kernel(
         wv_raw = [load_rows("wv_raw0", wv, 0, slice(0, N))]
         sc_rows = tile("sc_rows", [P, J], U8)
         nc.vector.tensor_copy(sc_rows[:], tab_sc[:].indirect(offsets[:]))
+        wv_raw.append(load_rows("wv_raw1", wv, 1, slice(0, N)))
         nc.vector.tensor_copy(both_rows[96:P, 0:J].bitcast(I32), sc_rows[96:P, :].bitcast(I32))
         for q in range(4):
             nc.sync.dma_start(planes[32 * q : 32 * q + 4, :, :].bitcast(I32), both_rows[96 + 8 * q : 96 + 8 * q + 8, :].bitcast(I32))
-        wv_raw.append(load_rows("wv_raw1", wv, 1, slice(0, N)))
         x_raw = [load_rows("x_raw0", x, 0, slice(0, M))]
 
         def quantize(name, rounded, cols):
@@ -179,11 +182,12 @@ def tile_list_kvt_ts_kernel(
         nc.vector.tensor_copy(v_q[0][:, :, P:BANK], parted(0)[:, :, P:BANK])
         wq_raw = {(a, 0): load_rows("wq_raw%d0" % a, wq, a, half[0]) for a in range(2)}
         gather_words(1)
-        for a in range(2):
-            wq_raw[a, 1] = load_rows("wq_raw%d1" % a, wq, a, half[1])
+        wq_raw[0, 1] = load_rows("wq_raw01", wq, 0, half[1])
+        wq_last = [load_rows("wq_last0", wq, 1, slice(KP, KP + KP // 2))]
         nc.vector.tensor_copy(v_q[1][:], parted(1))
         ts_g = tile("ts_g", [P, J], F32)
         nc.vector.tensor_copy(ts_g[:], ts_win[:].indirect(offsets[:]))
+        wq_last.append(load_rows("wq_last1", wq, 1, slice(KP + KP // 2, R)))
         order_wk(1)
 
         def round_wq(a, b):
@@ -236,8 +240,15 @@ def tile_list_kvt_ts_kernel(
         quantize_kr(0, 1)
         wq_q[0, 0] = quantize("wq00", rounded[:], KP)
         wq_q[1, 0] = quantize("wq10", round_wq(1, 0)[:], KP)
-        wq_q[0, 1] = quantize("wq01", round_wq(0, 1)[:], KP)
-        wq11_bf = round_wq(1, 1)
+        rounded = round_wq(0, 1)
+        wq11_bf = tile("wq11_bf", [P, KP * PACK], BF16)
+        for e in range(2):
+            nc.vector.tensor_copy(
+                wq11_bf[:].rearrange("p (t e g u i) -> p e t g i u", t=4, e=2, u=4, i=PACK)[:, e],
+                wq_last[e][:].rearrange("p i (g t u) -> p t g i u", t=4, u=4),
+            )
+            if e == 0:
+                wq_q[0, 1] = quantize("wq01", rounded[:], KP)
 
         results = []
 
@@ -316,19 +327,11 @@ def tile_list_kvt_ts_kernel(
                 stop=(b == 1),
             )
 
-        aside = []
-
         def score_out(acc, m, h):
             res = result()
-            dst = out_0[m * P : (m + 1) * P, h * BANK : (h + 1) * BANK]
-            if (m, h) in aside:
-                plain = result()
-                nc.scalar.copy(plain[:], acc[:])
-                nc.gpsimd.tensor_tensor(res[:], plain[:], ts_g[:, h * BANK : (h + 1) * BANK], MULT)
-                nc.scalar.dma_start(dst, res[:])
-            else:
-                nc.vector.tensor_tensor(res[:], acc[:], ts_g[:, h * BANK : (h + 1) * BANK], MULT)
-                nc.sync.dma_start(dst, res[:])
+            jcols = slice(h * BANK, (h + 1) * BANK)
+            nc.vector.tensor_tensor(res[:], acc[:], ts_g[:, jcols], MULT)
+            nc.sync.dma_start(out_0[m * P : (m + 1) * P, jcols], res[:])
 
         def scores(m, h):
             acc = bank([P, BANK])

@@ -32,12 +32,12 @@ def tile_list_kvt_ts_kernel(
         psum = ctx.enter_context(tc.psum_pool(name="psum", bufs=1))
 
         chains = [
-            [("wk_raw1", 4096), ("wk_raw0", 4096), ("wk_rows", R), ("wv_raw0", 4096)],
+            [("wk_raw0", 4096), ("wk_rows", R), ("wv_raw0", 4096)],
             [("wv_raw1", 4096), ("tab_sc", T)],
             [("sc_rows", J), ("x_raw0", 8192)],
-            [("x_raw1", 8192), ("both_rows", J + R)],
             [("wq_raw00", 8192), ("v_pair0", 2048), ("wq_raw10", 8192)],
-            [("wq_last0", 4096), ("tab_w", 4 * T), ("wq_raw01", 8192)],
+            [("wq_last0", 4096), ("v_pair1", 2048), ("wq_raw01", 8192)],
+            [("wk_raw1", 4096), ("tab_w", 4 * T), ("x_raw1", 8192)],
             [("ts_win", 4 * T)],
         ]
         where = {}
@@ -49,7 +49,7 @@ def tile_list_kvt_ts_kernel(
             end = end + LAP
         where["kr_bf00"] = where["wv_raw1"]
         for host, guests in [
-            ("wk_raw0", [("v_q0", 2048), ("v_pair1", 2048)]),
+            ("wk_raw0", [("v_q1", 2048)]),
             ("tab_w", [("wk_q1", 4096), ("kr00_q", 2048 - LAP), ("x0_bf", 4096 - LAP), ("x1_bf", 4096)]),
             ("x_raw0", [("wv_q", 2048)]),
             ("x_raw1", [("kr01_q", 2048), ("wq00_bf", 4096)]),
@@ -173,18 +173,17 @@ def tile_list_kvt_ts_kernel(
         def parted(h):
             return v_pair[h][:].bitcast(U16).rearrange("p (j d) -> p d j", d=2)
 
-        gather_words(0)
-        order_wk(0)
+        for h in range(2):
+            gather_words(h)
         wk_raw.append(load_wk(1))
         x_raw.append(load_rows("x_raw1", x, 1, slice(0, M)))
+        order_wk(0)
         v_q = [tile("v_q%d" % h, [P, 2, BANK], U16) for h in range(2)]
-        nc.vector.tensor_copy(v_q[0][:, :, 0:P], parted(0)[:, :, 0:P])
-        nc.vector.tensor_copy(v_q[0][:, :, P:BANK], parted(0)[:, :, P:BANK])
+        nc.vector.tensor_copy(v_q[0][:], parted(0))
         wq_raw = {(a, 0): load_rows("wq_raw%d0" % a, wq, a, half[0]) for a in range(2)}
-        gather_words(1)
+        nc.vector.tensor_copy(v_q[1][:], parted(1))
         wq_raw[0, 1] = load_rows("wq_raw01", wq, 0, half[1])
         wq_last = [load_rows("wq_last0", wq, 1, slice(KP, KP + KP // 2))]
-        nc.vector.tensor_copy(v_q[1][:], parted(1))
         ts_g = tile("ts_g", [P, J], F32)
         nc.vector.tensor_copy(ts_g[:], ts_win[:].indirect(offsets[:]))
         wq_last.append(load_rows("wq_last1", wq, 1, slice(KP + KP // 2, R)))

@@ -19,7 +19,7 @@ P = 128
 PACK = 4
 KP = P * PACK
 BANK = 512
-LAP = 64
+LAP = 256
 
 
 def tile_list_kvt_ts_kernel(
@@ -66,8 +66,8 @@ def tile_list_kvt_ts_kernel(
 
         def tile(name, shape, dtype):
             if name in where:
-                return shared.tile(shape, dtype, name=name, offset=where[name], align_bytes=64)
-            return sb.tile(shape, dtype, name=name, align_bytes=64)
+                return shared.tile(shape, dtype, name=name, offset=where[name], align_bytes=256)
+            return sb.tile(shape, dtype, name=name, align_bytes=256)
 
         taken = []
 

@@ -133,7 +133,7 @@ def tile_list_kvt_ts_kernel(
         nc.vector.tensor_copy(sc_rows[:], tab_sc[:].indirect(offsets[:]))
         wv_raw.append(load_rows("wv_raw1", wv, 1, slice(0, N)))
         nc.vector.tensor_copy(both_rows[96:P, 0:J].bitcast(I32), sc_rows[96:P, :].bitcast(I32))
-        for q in range(4):
+        for q in (0, 2, 1, 3):
             nc.sync.dma_start(planes[32 * q : 32 * q + 4, :, :].bitcast(I32), both_rows[96 + 8 * q : 96 + 8 * q + 8, :].bitcast(I32))
         x_raw = [load_rows("x_raw0", x, 0, slice(0, M))]
 

@@ -33,12 +33,10 @@ def tile_list_kvt_ts_kernel(
 
         chains = [
             [("wk_raw0", 4096), ("wk_rows", R), ("wv_raw0", 4096)],
-            [("wv_raw1", 4096), ("tab_sc", T)],
-            [("sc_rows", J), ("x_raw0", 8192)],
-            [("wq_raw00", 8192), ("v_pair0", 2048), ("wq_raw10", 8192)],
-            [("wq_last0", 4096), ("v_pair1", 2048), ("wq_raw01", 8192)],
+            [("wv_raw1", 4096), ("sc_rows", J), ("x_raw0", 8192)],
+            [("wq_raw00", 8192), ("v_pair0", 2048), ("tab_sc", T), ("v_pair1", 2048), ("wq_raw10", 8192)],
             [("wk_raw1", 4096), ("tab_w", 4 * T), ("x_raw1", 8192)],
-            [("ts_win", 4 * T)],
+            [("wq_raw01", 8192), ("ts_win", 4 * T), ("wq_last0", 4096)],
         ]
         where = {}
         end = 0
@@ -80,9 +78,9 @@ def tile_list_kvt_ts_kernel(
         offsets = tile("offsets", [P, J // 16], U16)
         nc.sync.dma_start(offsets[:], offs)
         tab_sc = tile("tab_sc", [P, T], U8)
-        nc.sync.dma_start(tab_sc[96:P, :].bitcast(I32), tab_scales.rearrange("a q t -> q a t").bitcast(I32))
+        nc.scalar.dma_start(tab_sc[96:P, :].bitcast(I32), tab_scales.rearrange("a q t -> q a t").bitcast(I32))
         wk_rows = tile("wk_rows", [P, R], U8)
-        nc.sync.dma_start(wk_rows[96:P, :].bitcast(I32), wk_scales.rearrange("a q r -> q a r").bitcast(I32))
+        nc.scalar.dma_start(wk_rows[96:P, :].bitcast(I32), wk_scales.rearrange("a q r -> q a r").bitcast(I32))
 
         def load_rows(name, src, a, cols):
             raw = tile(name, [P, PACK, cols.stop - cols.start], F32)
@@ -131,8 +129,8 @@ def tile_list_kvt_ts_kernel(
         wv_raw = [load_rows("wv_raw0", wv, 0, slice(0, N))]
         sc_rows = tile("sc_rows", [P, J], U8)
         nc.vector.tensor_copy(sc_rows[:], tab_sc[:].indirect(offsets[:]))
-        wv_raw.append(load_rows("wv_raw1", wv, 1, slice(0, N)))
         nc.vector.tensor_copy(both_rows[96:P, 0:J].bitcast(I32), sc_rows[96:P, :].bitcast(I32))
+        wv_raw.append(load_rows("wv_raw1", wv, 1, slice(0, N)))
         for q in (0, 2, 1, 3):
             nc.sync.dma_start(planes[32 * q : 32 * q + 4, :, :].bitcast(I32), both_rows[96 + 8 * q : 96 + 8 * q + 8, :].bitcast(I32))
         x_raw = [load_rows("x_raw0", x, 0, slice(0, M))]
@@ -180,12 +178,13 @@ def tile_list_kvt_ts_kernel(
         order_wk(0)
         v_q = [tile("v_q%d" % h, [P, 2, BANK], U16) for h in range(2)]
         nc.vector.tensor_copy(v_q[0][:], parted(0))
-        wq_raw = {(a, 0): load_rows("wq_raw%d0" % a, wq, a, half[0]) for a in range(2)}
+        wq_raw = {(0, 0): load_rows("wq_raw00", wq, 0, half[0])}
         nc.vector.tensor_copy(v_q[1][:], parted(1))
-        wq_raw[0, 1] = load_rows("wq_raw01", wq, 0, half[1])
-        wq_last = [load_rows("wq_last0", wq, 1, slice(KP, KP + KP // 2))]
+        wq_raw[1, 0] = load_rows("wq_raw10", wq, 1, half[0])
         ts_g = tile("ts_g", [P, J], F32)
         nc.vector.tensor_copy(ts_g[:], ts_win[:].indirect(offsets[:]))
+        wq_raw[0, 1] = load_rows("wq_raw01", wq, 0, half[1])
+        wq_last = [load_rows("wq_last0", wq, 1, slice(KP, KP + KP // 2))]
         wq_last.append(load_rows("wq_last1", wq, 1, slice(KP + KP // 2, R)))
         order_wk(1)
 

@@ -122,8 +122,8 @@ def tile_list_kvt_ts_kernel(
 
         both_rows = tile("both_rows", [P, J + R], U8)
         nc.vector.tensor_copy(
-            both_rows[96:P, J:].bitcast(I32).rearrange("p (b t g) -> p b g t", t=4, g=32),
-            wk_rows[96:P, :].bitcast(I32).rearrange("p (b g t) -> p b g t", t=4, g=32),
+            both_rows[96:P, J:].bitcast(I32).rearrange("p (b t g w) -> p b t g w", t=4, g=16, w=2),
+            wk_rows[96:P, :].bitcast(I32).rearrange("p (b g t w) -> p b t g w", t=4, g=16, w=2),
         )
         wk_raw = [load_wk(0)]
         wv_raw = [load_rows("wv_raw0", wv, 0, slice(0, N))]
@@ -142,7 +142,7 @@ def tile_list_kvt_ts_kernel(
             return codes, scales
 
         def round_plain(copy, rounded, raw):
-            copy(rounded.rearrange("p (c u i) -> p c i u", u=4, i=PACK), raw.rearrange("p i (c u) -> p c i u", u=4))
+            copy(rounded.rearrange("p (c u i) -> p c i u", u=8, i=PACK), raw.rearrange("p i (c u) -> p c i u", u=8))
 
         def round_x(a):
             rounded = tile("x%d_bf" % a, [P, M * PACK], BF16)
@@ -154,8 +154,8 @@ def tile_list_kvt_ts_kernel(
         def order_wk(b):
             wk_q[b] = tile("wk_q%d" % b, [P, 2, KP], I32)
             nc.vector.tensor_copy(
-                wk_q[b][:].rearrange("p a (t g u) -> p a t g u", t=4, u=4),
-                wk_raw[b][:].rearrange("p a (g t u) -> p a t g u", t=4, u=4),
+                wk_q[b][:].rearrange("p a (t g u) -> p a t g u", t=4, u=8),
+                wk_raw[b][:].rearrange("p a (g t u) -> p a t g u", t=4, u=8),
             )
 
         x_q = {}
@@ -191,8 +191,8 @@ def tile_list_kvt_ts_kernel(
         def round_wq(a, b):
             rounded = tile("wq%d%d_bf" % (a, b), [P, KP * PACK], BF16)
             nc.vector.tensor_copy(
-                rounded[:].rearrange("p (t g u i) -> p t g i u", t=4, u=4, i=PACK),
-                wq_raw[a, b][:].rearrange("p i (g t u) -> p t g i u", t=4, u=4),
+                rounded[:].rearrange("p (t g u i) -> p t g i u", t=4, u=8, i=PACK),
+                wq_raw[a, b][:].rearrange("p i (g t u) -> p t g i u", t=4, u=8),
             )
             return rounded
 
@@ -242,8 +242,8 @@ def tile_list_kvt_ts_kernel(
         wq11_bf = tile("wq11_bf", [P, KP * PACK], BF16)
         for e in range(2):
             nc.vector.tensor_copy(
-                wq11_bf[:].rearrange("p (t e g u i) -> p e t g i u", t=4, e=2, u=4, i=PACK)[:, e],
-                wq_last[e][:].rearrange("p i (g t u) -> p t g i u", t=4, u=4),
+                wq11_bf[:].rearrange("p (t e g u i) -> p e t g i u", t=4, e=2, u=8, i=PACK)[:, e],
+                wq_last[e][:].rearrange("p i (g t u) -> p t g i u", t=4, u=8),
             )
             if e == 0:
                 wq_q[0, 1] = quantize("wq01", rounded[:], KP)

from contextlib import ExitStack

import concourse.mybir as mybir

K, R, M, N, T, J = 1024, 1024, 512, 256, 4096, 1024
FLOPS = 2 * (K * R * M + K * R * J + R * M * J + K * N * J)

F32 = mybir.dt.float32
BF16 = mybir.dt.bfloat16
I32 = mybir.dt.int32
U32 = mybir.dt.uint32
U16 = mybir.dt.uint16
U8 = mybir.dt.uint8
FP8X4 = mybir.dt.float8_e4m3fn_x4
FP4X4 = mybir.dt.float4_e2m1fn_x4
MULT = mybir.AluOpType.mult

P = 128
PACK = 4
KP = P * PACK
BANK = 512
LAP = 256


def tile_list_kvt_ts_kernel(
    tc, tab_words, tab_scales, x, wq, wk_words, wk_scales, wv, ts, offs, out_0, out_1
):
    nc = tc.nc
    with ExitStack() as ctx:
        sb = ctx.enter_context(tc.tile_pool(name="sb", bufs=1))
        shared = ctx.enter_context(tc.tile_pool(name="shared", bufs=1))
        psum = ctx.enter_context(tc.psum_pool(name="psum", bufs=1))

        chains = [
            [("wk_raw0", 4096), ("wk_rows", R), ("wv_raw0", 4096)],
            [("wv_raw1", 4096), ("sc_rows", J), ("x_raw0", 8192)],
            [("wq_raw00", 8192), ("v_pair0", 2048), ("tab_sc", T), ("v_pair1", 2048), ("wq_raw10", 8192)],
            [("wk_raw1", 4096), ("tab_w", 4 * T), ("x_raw1", 8192)],
            [("wq_raw01", 8192), ("ts_win", 4 * T), ("wq_last0", 4096)],
        ]
        where = {}
        end = 0
        for chain in chains:
            for name, size in chain:
                where[name] = end
                end = end + size - LAP
            end = end + LAP
        where["kr_bf00"] = where["wv_raw1"]
        for host, guests in [
            ("wk_raw0", [("v_q1", 2048)]),
            ("tab_w", [("wk_q1", 4096), ("kr00_q", 2048 - LAP), ("x0_bf", 4096 - LAP), ("x1_bf", 4096)]),
            ("x_raw0", [("wv_q", 2048)]),
            ("x_raw1", [("kr01_q", 2048), ("wq00_bf", 4096)]),
            ("wq_raw00", [("wq10_bf", 4096)]),
            ("wq_raw10", [("wq01_bf", 4096)]),
            ("ts_win", [("qr0_q", 2048 - LAP), ("wq_last1", 4096 - LAP), ("kr11_q", 2048)]),
            ("wq_last1", [("kr10_q", 2048)]),
        ]:
            end = where[host] + LAP
            for name, size in guests:
                where[name] = end
                end = end + size
        where["wq11_bf"] = where["wq10_bf"]

        def tile(name, shape, dtype):
            if name in where:
                return shared.tile(shape, dtype, name=name, offset=where[name], align_bytes=256)
            return sb.tile(shape, dtype, name=name, align_bytes=256)

        taken = []

        def bank(shape):
            taken.append(len(taken) % 8)
            return psum.tile(shape, F32, name="bank%d" % len(taken), offset=2048 * taken[-1])

        ts_row = tile("ts_row", [P, T // P], F32)
        nc.sync.dma_start(ts_row[:], ts[0, :].rearrange("(n c) -> n c", n=P))
        offsets = tile("offsets", [P, J // 16], U16)
        nc.sync.dma_start(offsets[:], offs)
        tab_sc = tile("tab_sc", [P, T], U8)
        nc.scalar.dma_start(tab_sc[96:P, :].bitcast(I32), tab_scales.rearrange("a q t -> q a t").bitcast(I32))
        wk_rows = tile("wk_rows", [P, R], U8)
        nc.scalar.dma_start(wk_rows[96:P, :].bitcast(I32), wk_scales.rearrange("a q r -> q a r").bitcast(I32))

        def load_rows(name, src, a, cols):
            raw = tile(name, [P, PACK, cols.stop - cols.start], F32)
            nc.sync.dma_start(raw[:], src[a * KP : (a + 1) * KP, cols].rearrange("(p i) c -> p i c", i=PACK))
            return raw

        def load_wk(b):
            raw = tile("wk_raw%d" % b, [P, 2, KP], I32)
            nc.sync.dma_start(raw[:], wk_words[:, :, b * KP : (b + 1) * KP, :].rearrange("a p r i -> p a (r i)").bitcast(I32))
            return raw

        tab_w = tile("tab_w", [P, T], U32)
        nc.sync.dma_start(tab_w[:].bitcast(I32), tab_words[0].rearrange("p t b -> p (t b)").bitcast(I32))

        ones = tile("ones", [P, P], F32)
        ident = tile("ident", [P, P], F32)
        nc.vector.memset(ones[:], 1.0)
        nc.gpsimd.affine_select(
            out=ident[:],
            in_=ones[:],
            pattern=[[-1, P]],
            compare_op=mybir.AluOpType.is_equal,
            fill=0.0,
            base=0,
            channel_multiplier=1,
        )
        nc.vector.memset(tab_sc[0:96, :].bitcast(I32), 0)
        planes = tile("planes", [P, 2, J + R], U8)
        nc.vector.memset(planes[:].rearrange("p a j -> p (a j)").bitcast(I32), 0)

        ts_win = tile("ts_win", [P, T], F32)
        ts_by_n = ts_win[:].rearrange("p (n c) -> p n c", n=P)
        for g in range(T // P // 4):
            acc = bank([P, 4, P])
            for c in range(4):
                col = 4 * g + c
                nc.tensor.transpose(acc[:, c, :], ts_row[:, col : col + 1].to_broadcast([P, P]), ident[:])
            nc.scalar.copy(ts_by_n[:, :, 4 * g : 4 * g + 4], acc[:].rearrange("p c n -> p n c"))

        both_rows = tile("both_rows", [P, J + R], U8)
        nc.vector.tensor_copy(
            both_rows[96:P, J:].bitcast(I32).rearrange("p (b t g w) -> p b t g w", t=4, g=16, w=2),
            wk_rows[96:P, :].bitcast(I32).rearrange("p (b g t w) -> p b t g w", t=4, g=16, w=2),
        )
        wk_raw = [load_wk(0)]
        wv_raw = [load_rows("wv_raw0", wv, 0, slice(0, N))]
        sc_rows = tile("sc_rows", [P, J], U8)
        nc.vector.tensor_copy(sc_rows[:], tab_sc[:].indirect(offsets[:]))
        nc.vector.tensor_copy(both_rows[96:P, 0:J].bitcast(I32), sc_rows[96:P, :].bitcast(I32))
        wv_raw.append(load_rows("wv_raw1", wv, 1, slice(0, N)))
        for q in (0, 2, 1, 3):
            nc.sync.dma_start(planes[32 * q : 32 * q + 4, :, :].bitcast(I32), both_rows[96 + 8 * q : 96 + 8 * q + 8, :].bitcast(I32))
        x_raw = [load_rows("x_raw0", x, 0, slice(0, M))]

        def quantize(name, rounded, cols):
            codes = tile(name + "_q", [P, cols], U32)
            scales = tile(name + "_s", [P, cols], U8)
            nc.vector.quantize_mx(out=codes[:].bitcast(FP8X4), scales=scales[:], in_=rounded)
            return codes, scales

        def round_plain(copy, rounded, raw):
            copy(rounded.rearrange("p (c u i) -> p c i u", u=8, i=PACK), raw.rearrange("p i (c u) -> p c i u", u=8))

        def round_x(a):
            rounded = tile("x%d_bf" % a, [P, M * PACK], BF16)
            round_plain(nc.vector.tensor_copy, rounded[:], x_raw[a][:])
            return rounded

        wk_q = {}

        def order_wk(b):
            wk_q[b] = tile("wk_q%d" % b, [P, 2, KP], I32)
            nc.vector.tensor_copy(
                wk_q[b][:].rearrange("p a (t g u) -> p a t g u", t=4, u=8),
                wk_raw[b][:].rearrange("p a (g t u) -> p a t g u", t=4, u=8),
            )

        x_q = {}
        wq_q = {}
        half = [slice(0, KP), slice(KP, 2 * KP)]

        v_pair = {}

        def gather_words(h):
            v_pair[h] = tile("v_pair%d" % h, [P, BANK], U32)
            nc.vector.tensor_copy(v_pair[h][:], tab_w[:].indirect(offsets[:, 32 * h : 32 * (h + 1)]))

        def parted(h):
            return v_pair[h][:].bitcast(U16).rearrange("p (j d) -> p d j", d=2)

        for h in range(2):
            gather_words(h)
        wk_raw.append(load_wk(1))
        x_raw.append(load_rows("x_raw1", x, 1, slice(0, M)))
        order_wk(0)
        v_q = [tile("v_q%d" % h, [P, 2, BANK], U16) for h in range(2)]
        nc.vector.tensor_copy(v_q[0][:], parted(0))
        wq_raw = {(0, 0): load_rows("wq_raw00", wq, 0, half[0])}
        nc.vector.tensor_copy(v_q[1][:], parted(1))
        wq_raw[1, 0] = load_rows("wq_raw10", wq, 1, half[0])
        ts_g = tile("ts_g", [P, J], F32)
        nc.vector.tensor_copy(ts_g[:], ts_win[:].indirect(offsets[:]))
        wq_raw[0, 1] = load_rows("wq_raw01", wq, 0, half[1])
        wq_last = [load_rows("wq_last0", wq, 1, slice(KP, KP + KP // 2))]
        wq_last.append(load_rows("wq_last1", wq, 1, slice(KP + KP // 2, R)))
        order_wk(1)

        def round_wq(a, b):
            rounded = tile("wq%d%d_bf" % (a, b), [P, KP * PACK], BF16)
            nc.vector.tensor_copy(
                rounded[:].rearrange("p (t g u i) -> p t g i u", t=4, u=8, i=PACK),
                wq_raw[a, b][:].rearrange("p i (g t u) -> p t g i u", t=4, u=8),
            )
            return rounded

        kr_bf = {(b, h): tile("kr_bf%d%d" % (b, h), [P, BANK, PACK], BF16) for b in range(2) for h in range(2)}

        def kr_bank(b, h, c):
            acc = bank([P, 4, P])
            cols = slice(c * P, (c + 1) * P)
            jcols = slice(h * BANK + c * P, h * BANK + (c + 1) * P)
            for a in range(2):
                for t in range(4):
                    nc.tensor.matmul_mx(
                        out=acc[:, t, :],
                        lhsT=wk_q[b][:, a, t * P : (t + 1) * P].bitcast(FP8X4),
                        lhsT_scale=planes[:, a, J + b * KP + t * P : J + b * KP + (t + 1) * P],
                        rhs=v_q[h][:, a, cols].bitcast(FP4X4),
                        rhs_scale=planes[:, a, jcols],
                        start=(a == 0 and t == 0),
                        stop=(a == 1 and t == 3),
                    )
            nc.scalar.copy(kr_bf[b, h][:, cols, :], acc[:].rearrange("p t n -> p n t"))

        kr_q = {}

        def quantize_kr(b, h):
            kr_q[b, h] = quantize("kr%d%d" % (b, h), kr_bf[b, h][:].rearrange("p n t -> p (n t)"), BANK)

        wv_bf = tile("wv_bf", [P, 2, N * PACK], BF16)
        for a in range(2):
            round_plain(nc.scalar.copy, wv_bf[:, a, :], wv_raw[a][:])
        rounded = round_x(0)
        wv_q = quantize("wv", wv_bf[:].rearrange("p a c -> p (a c)"), 2 * N)
        x_q[0] = quantize("x0", rounded[:], M)
        x1_bf = round_x(1)
        for b in range(2):
            for h in range(2):
                for c in range(4):
                    kr_bank(b, h, c)

        quantize_kr(0, 0)
        x_q[1] = quantize("x1", x1_bf[:], M)
        rounded = round_wq(0, 0)
        quantize_kr(0, 1)
        wq_q[0, 0] = quantize("wq00", rounded[:], KP)
        wq_q[1, 0] = quantize("wq10", round_wq(1, 0)[:], KP)
        rounded = round_wq(0, 1)
        wq11_bf = tile("wq11_bf", [P, KP * PACK], BF16)
        for e in range(2):
            nc.vector.tensor_copy(
                wq11_bf[:].rearrange("p (t e g u i) -> p e t g i u", t=4, e=2, u=8, i=PACK)[:, e],
                wq_last[e][:].rearrange("p i (g t u) -> p t g i u", t=4, u=8),
            )
            if e == 0:
                wq_q[0, 1] = quantize("wq01", rounded[:], KP)

        results = []

        def result():
            results.append(tile("res%d" % len(results), [P, BANK], F32))
            return results[-1]

        def values(n, h):
            res = result()
            acc = bank([P, BANK])
            cols = slice(h * BANK, (h + 1) * BANK)
            for a in range(2):
                ncols = slice(a * N + n * P, a * N + (n + 1) * P)
                nc.tensor.matmul_mx(
                    out=acc[:],
                    lhsT=wv_q[0][:, ncols].bitcast(FP8X4),
                    lhsT_scale=wv_q[1][:, ncols],
                    rhs=v_q[h][:, a, :].bitcast(FP4X4),
                    rhs_scale=planes[:, a, cols],
                    start=(a == 0),
                    stop=(a == 1),
                )
            nc.scalar.copy(res[:], acc[:])
            nc.sync.dma_start(out_1[n * P : (n + 1) * P, cols], res[:])

        for n in range(2):
            for h in range(2):
                values(n, h)

        qr_bf = [tile("qr_bf%d" % b, [P, M, PACK], BF16) for b in range(2)]

        def qr_pass(acc, a, b, m):
            cols = slice(m * P, (m + 1) * P)
            for t in range(4):
                nc.tensor.matmul_mx(
                    out=acc[:, t, :],
                    lhsT=wq_q[a, b][0][:, t * P : (t + 1) * P].bitcast(FP8X4),
                    lhsT_scale=wq_q[a, b][1][:, t * P : (t + 1) * P],
                    rhs=x_q[a][0][:, cols].bitcast(FP8X4),
                    rhs_scale=x_q[a][1][:, cols],
                    start=(a == 0 and t == 0),
                    stop=(a == 1 and t == 3),
                )

        def qr_out(acc, b, m):
            nc.scalar.copy(qr_bf[b][:, m * P : (m + 1) * P, :], acc[:].rearrange("p t n -> p n t"))

        for m in range(4):
            acc = bank([P, 4, P])
            qr_pass(acc, 0, 0, m)
            qr_pass(acc, 1, 0, m)
            qr_out(acc, 0, m)
        accs = [bank([P, 4, P]) for m in range(4)]
        for m in range(4):
            qr_pass(accs[m], 0, 1, m)
        wq_q[1, 1] = quantize("wq11", wq11_bf[:], KP)
        for m in range(4):
            qr_pass(accs[m], 1, 1, m)
            qr_out(accs[m], 1, m)
        qr0 = quantize("qr0", qr_bf[0][:].rearrange("p n t -> p (n t)"), M)
        quantize_kr(1, 0)
        qr_q = {(0, m): (qr0[0][:, m * P : (m + 1) * P], qr0[1][:, m * P : (m + 1) * P]) for m in range(4)}

        def quantize_qr1(m):
            codes, scales = quantize("qr1%d" % m, qr_bf[1][:, m * P : (m + 1) * P, :].rearrange("p n t -> p (n t)"), P)
            qr_q[1, m] = (codes[:], scales[:])

        def score_pass(acc, b, m, h):
            nc.tensor.matmul_mx(
                out=acc[:],
                lhsT=qr_q[b, m][0].bitcast(FP8X4),
                lhsT_scale=qr_q[b, m][1],
                rhs=kr_q[b, h][0][:].bitcast(FP8X4),
                rhs_scale=kr_q[b, h][1][:],
                start=(b == 0),
                stop=(b == 1),
            )

        def score_out(acc, m, h):
            res = result()
            jcols = slice(h * BANK, (h + 1) * BANK)
            nc.vector.tensor_tensor(res[:], acc[:], ts_g[:, jcols], MULT)
            nc.sync.dma_start(out_0[m * P : (m + 1) * P, jcols], res[:])

        def scores(m, h):
            acc = bank([P, BANK])
            for b in range(2):
                score_pass(acc, b, m, h)
            score_out(acc, m, h)

        early = [bank([P, BANK]) for m in range(4)]
        for m in range(4):
            score_pass(early[m], 0, m, 0)
        for m in range(4):
            quantize_qr1(m)
            if m == 0:
                quantize_kr(1, 1)
            score_pass(early[m], 1, m, 0)
            score_out(early[m], m, 0)
            scores(m, 1)
